import numpy as np
import ml_dtypes


def mxq(x, axis, fmt="e4m3"):
    dtype, down = {"e4m3": (ml_dtypes.float8_e4m3fn, 7), "e5m2": (ml_dtypes.float8_e5m2, 14)}[fmt]
    v = np.moveaxis(np.asarray(x, np.float32).astype(ml_dtypes.bfloat16).astype(np.float64), axis, -1)
    blocks = v.reshape(v.shape[:-1] + (-1, 32))
    amax = np.abs(blocks).max(-1, keepdims=True)
    byte = np.maximum(np.where(amax > 0, np.frexp(amax)[1] - 1 + 127, 0) - down, 1)
    scale = np.exp2(byte - 127.0)
    codes = (blocks / scale).astype(np.float32).astype(dtype).astype(np.float64)
    return np.moveaxis((codes * scale).reshape(v.shape), -1, axis)


WIDE = False


def mx_kscale(k):
    if not WIDE:
        return np.ones(k)
    levels = np.array([10, -10, 5, -5, 0])
    if k % 512:
        return np.exp2(np.random.permutation(np.resize(levels, k // 32))).repeat(32)
    a = np.empty((k // 512, 16))
    for p in range(k // 512):
        a[p, :8] = np.random.permutation(np.resize(levels, 8))
        for g in range(8):
            far = levels[np.abs(levels - a[p, g]) >= 10]
            a[p, g + 8] = far[np.random.randint(len(far))]
    return np.exp2(a.ravel()).repeat(32)


def f64(x):
    return np.asarray(x).astype(np.float64)


def striped(idx):
    return np.tile(idx.reshape(-1, 16).T, (8, 1)).astype(np.uint16)


def unstriped(offs):
    return offs[:16].T.reshape(-1).astype(np.int64)


K, T, S, N, U = 512, 2048, 512, 128, 1024
P = 2 ** 7


def setup_inputs():
    n = np.random.standard_normal
    s = mx_kscale(K)[:, None]
    return {
        "xT": (n((K, T)) * s).astype(np.float32),
        "mem": n((N, U)).astype(np.float32),
        "w1": (n((K, N)) / np.sqrt(K) / s).astype(np.float32),
        "old": np.tile(np.random.uniform(0.5, 0.95, S), (P, 1)).astype(np.float32),
        "new": np.tile(np.random.uniform(0.05, 0.5, S), (P, 1)).astype(np.float32),
        "offs": striped(np.random.permutation(T)[:S]),
        "slot": striped(np.random.permutation(U)[:S]),
    }


def reference(xT, mem, w1, old, new, offs, slot):
    xq = mxq(f64(xT)[:, unstriped(offs)], 0, "e4m3")
    y = mxq(f64(w1), 0, "e4m3").T @ xq
    out = f64(mem).copy()
    out[:, unstriped(slot)] = f64(mem)[:, unstriped(slot)] * f64(old)[:1] + y * f64(new)[:1]
    return out

@@ -1,0 +1,118 @@
+from contextlib import ExitStack
+
+import concourse.mybir as mybir
+from concourse.masks import make_identity
+
+K, T, S, N, U = 512, 2048, 512, 128, 1024
+P = 128
+PACK = 4
+FLOPS = 2 * K * N * S
+
+F32 = mybir.dt.float32
+BF16 = mybir.dt.bfloat16
+U32 = mybir.dt.uint32
+U16 = mybir.dt.uint16
+U8 = mybir.dt.uint8
+FP8X4 = mybir.dt.float8_e4m3fn_x4
+MULT = mybir.AluOpType.mult
+ADD = mybir.AluOpType.add
+COPY = mybir.ActivationFunctionType.Copy
+
+HALF = S // 2
+CHUNK = 512
+
+
+def tile_picked_ema_none_e_kernel(tc, xT, mem, w1, old, new, offs, slot, out):
+    nc = tc.nc
+    with ExitStack() as ctx:
+        keep = ctx.enter_context(tc.tile_pool(name="keep", bufs=1))
+        psum = ctx.enter_context(tc.psum_pool(name="psum", bufs=1))
+
+        x_rows = xT.rearrange("(p j) t -> p j t", j=PACK)
+        planes = [keep.tile([P, T], F32, name=f"plane{j}") for j in range(PACK)]
+
+        old_col = keep.tile([P, PACK], F32, name="old_col")
+        nc.scalar.dma_start(out=old_col[:], in_=old[0:1, :].rearrange("o (p c) -> (o p) c", c=PACK))
+        new_col = keep.tile([P, PACK], F32, name="new_col")
+        nc.scalar.dma_start(out=new_col[:], in_=new[0:1, :].rearrange("o (p c) -> (o p) c", c=PACK))
+        offs_sb = keep.tile([P, S // 16], U16, name="offs_sb")
+        nc.sync.dma_start(offs_sb[:], offs)
+        nc.sync.dma_start(out=planes[2][:], in_=x_rows[:, 2, :])
+        slot_sb = keep.tile([P, S // 16], U16, name="slot_sb")
+        nc.sync.dma_start(slot_sb[:], slot)
+        mem_sb = keep.tile([P, U], F32, name="mem_sb")
+        nc.sync.dma_start(out=mem_sb[:], in_=mem)
+        w_raw = keep.tile([P, PACK, N], F32, name="w_raw")
+        for j in (0, 1):
+            nc.sync.dma_start(out=planes[j][:], in_=x_rows[:, j, :])
+        for c0 in range(0, T, CHUNK):
+            nc.sync.dma_start(out=planes[3][:, c0 : c0 + CHUNK], in_=x_rows[:, 3, c0 : c0 + CHUNK])
+        nc.sync.dma_start(out=w_raw[:], in_=w1.rearrange("(p j) m -> p j m", j=PACK))
+
+        ident = keep.tile([P, P], F32, name="ident")
+        make_identity(nc, ident[:])
+
+        def spread(col, name):
+            bank = psum.tile([P, PACK, P], F32, name=name + "_bank")
+            for c in range(PACK):
+                nc.tensor.transpose(bank[:, c, :], col[:, c : c + 1].to_broadcast([P, P]), ident[:])
+            full = keep.tile([P, S], F32, name=name)
+            nc.scalar.copy(out=full[:].rearrange("p (k c) -> p k c", c=PACK), in_=bank[:].rearrange("p c k -> p k c"))
+            return full
+
+        old_all = spread(old_col, "old_all")
+        new_all = spread(new_col, "new_all")
+
+        picked = keep.tile([P, S, PACK], BF16, name="picked", align_bytes=64)
+        first = slice(0, HALF)
+        second = slice(HALF, S)
+        offs_first = offs_sb[:, 0 : HALF // 16]
+        offs_second = offs_sb[:, HALF // 16 : S // 16]
+
+        nc.vector.tensor_copy(picked[:, first, 2], planes[2][:].indirect(offs_first))
+        rounded2 = keep.tile([P, T], BF16, name="rounded2")
+        nc.scalar.copy(out=rounded2[:], in_=planes[2][:])
+        nc.scalar.activation(picked[:, second, 2], rounded2[:].indirect(offs_second), COPY)
+
+        kept = keep.tile([P, S], F32, name="kept")
+        nc.vector.tensor_tensor(kept[:], mem_sb[:].indirect(slot_sb[:]), old_all[:], MULT)
+        result = keep.tile([P, U], F32, name="result")
+        nc.scalar.copy(out=result[:], in_=mem_sb[:])
+
+        for j in (0, 1):
+            nc.vector.tensor_copy(picked[:, :, j], planes[j][:].indirect(offs_sb[:]))
+
+        rounded3 = keep.tile([P, T], BF16, name="rounded3")
+        for c0 in range(0, T, CHUNK):
+            nc.scalar.copy(out=rounded3[:, c0 : c0 + CHUNK], in_=planes[3][:, c0 : c0 + CHUNK])
+        nc.vector.tensor_copy(picked[:, first, 3], planes[3][:].indirect(offs_first))
+        nc.scalar.activation(picked[:, second, 3], rounded3[:].indirect(offs_second), COPY)
+
+        w_grouped = keep.tile([P, N, PACK], BF16, name="w_grouped", align_bytes=64)
+        nc.vector.tensor_copy(out=w_grouped[:], in_=w_raw[:].rearrange("p j m -> p m j"))
+        w_codes = keep.tile([P, N], U32, name="w_codes", align_bytes=64)
+        w_scales = keep.tile([P, N], U8, name="w_scales", align_bytes=64)
+
+        x_codes = [keep.tile([P, HALF], U32, name=f"x_codes{h}", align_bytes=64) for h in range(2)]
+        x_scales = [keep.tile([P, HALF], U8, name=f"x_scales{h}", align_bytes=64) for h in range(2)]
+        halves = (first, second)
+
+        def quantise_x(h):
+            nc.vector.quantize_mx(out=x_codes[h][:].bitcast(FP8X4), scales=x_scales[h][:], in_=picked[:, halves[h], :].rearrange("p s j -> p (s j)"))
+
+        quantise_x(0)
+        nc.vector.quantize_mx(out=w_codes[:].bitcast(FP8X4), scales=w_scales[:], in_=w_grouped[:].rearrange("p m j -> p (m j)"))
+        quantise_x(1)
+        banks = []
+        for h in range(2):
+            y_bank = psum.tile([P, HALF], F32, name=f"y_bank{h}")
+            nc.tensor.matmul_mx(out=y_bank[:], lhsT=w_codes[:].bitcast(FP8X4), lhsT_scale=w_scales[:], rhs=x_codes[h][:].bitcast(FP8X4), rhs_scale=x_scales[h][:], start=True, stop=True)
+            banks.append(y_bank)
+        added = []
+        for h in range(2):
+            y_new = keep.tile([P, HALF], F32, name=f"y_new{h}")
+            nc.vector.tensor_tensor(y_new[:], banks[h][:], new_all[:, halves[h]], MULT)
+            added.append(y_new)
+        for h in range(2):
+            nc.vector.tensor_tensor(result[:].indirect(slot_sb[:, h * HALF // 16 : (h + 1) * HALF // 16]), kept[:, halves[h]], added[h][:], ADD)
+        nc.sync.dma_start(out=out, in_=result[:])

@@ -19,7 +19,7 @@ ADD = mybir.AluOpType.add
 COPY = mybir.ActivationFunctionType.Copy
 
 HALF = S // 2
-CHUNK = 512
+CHUNKS = ((0, 1024), (1024, 1536), (1536, 1792), (1792, 2048))
 
 
 def tile_picked_ema_none_e_kernel(tc, xT, mem, w1, old, new, offs, slot, out):
@@ -36,18 +36,18 @@ def tile_picked_ema_none_e_kernel(tc, xT, mem, w1, old, new, offs, slot, out):
         new_col = keep.tile([P, PACK], F32, name="new_col")
         nc.scalar.dma_start(out=new_col[:], in_=new[0:1, :].rearrange("o (p c) -> (o p) c", c=PACK))
         offs_sb = keep.tile([P, S // 16], U16, name="offs_sb")
-        nc.sync.dma_start(offs_sb[:], offs)
         nc.sync.dma_start(out=planes[2][:], in_=x_rows[:, 2, :])
+        nc.sync.dma_start(offs_sb[:], offs)
         slot_sb = keep.tile([P, S // 16], U16, name="slot_sb")
         nc.sync.dma_start(slot_sb[:], slot)
         mem_sb = keep.tile([P, U], F32, name="mem_sb")
         nc.sync.dma_start(out=mem_sb[:], in_=mem)
         w_raw = keep.tile([P, PACK, N], F32, name="w_raw")
+        nc.sync.dma_start(out=w_raw[:], in_=w1.rearrange("(p j) m -> p j m", j=PACK))
         for j in (0, 1):
             nc.sync.dma_start(out=planes[j][:], in_=x_rows[:, j, :])
-        for c0 in range(0, T, CHUNK):
-            nc.sync.dma_start(out=planes[3][:, c0 : c0 + CHUNK], in_=x_rows[:, 3, c0 : c0 + CHUNK])
-        nc.sync.dma_start(out=w_raw[:], in_=w1.rearrange("(p j) m -> p j m", j=PACK))
+        for c0, c1 in CHUNKS:
+            nc.sync.dma_start(out=planes[3][:, c0:c1], in_=x_rows[:, 3, c0:c1])
 
         ident = keep.tile([P, P], F32, name="ident")
         make_identity(nc, ident[:])
@@ -83,8 +83,11 @@ def tile_picked_ema_none_e_kernel(tc, xT, mem, w1, old, new, offs, slot, out):
             nc.vector.tensor_copy(picked[:, :, j], planes[j][:].indirect(offs_sb[:]))
 
         rounded3 = keep.tile([P, T], BF16, name="rounded3")
-        for c0 in range(0, T, CHUNK):
-            nc.scalar.copy(out=rounded3[:, c0 : c0 + CHUNK], in_=planes[3][:, c0 : c0 + CHUNK])
+        for i, (c0, c1) in enumerate(CHUNKS):
+            if i > 0:
+                nc.vector.tensor_copy(out=rounded3[:, c0:c1], in_=planes[3][:, c0:c1])
+            else:
+                nc.scalar.copy(out=rounded3[:, c0:c1], in_=planes[3][:, c0:c1])
         nc.vector.tensor_copy(picked[:, first, 3], planes[3][:].indirect(offs_first))
         nc.scalar.activation(picked[:, second, 3], rounded3[:].indirect(offs_second), COPY)
 

@@ -40,12 +40,12 @@ def tile_picked_ema_none_e_kernel(tc, xT, mem, w1, old, new, offs, slot, out):
         nc.sync.dma_start(offs_sb[:], offs)
         slot_sb = keep.tile([P, S // 16], U16, name="slot_sb")
         nc.sync.dma_start(slot_sb[:], slot)
+        nc.sync.dma_start(out=planes[0][:], in_=x_rows[:, 0, :])
         mem_sb = keep.tile([P, U], F32, name="mem_sb")
         nc.sync.dma_start(out=mem_sb[:], in_=mem)
+        nc.sync.dma_start(out=planes[1][:], in_=x_rows[:, 1, :])
         w_raw = keep.tile([P, PACK, N], F32, name="w_raw")
         nc.sync.dma_start(out=w_raw[:], in_=w1.rearrange("(p j) m -> p j m", j=PACK))
-        for j in (0, 1):
-            nc.sync.dma_start(out=planes[j][:], in_=x_rows[:, j, :])
         for c0, c1 in CHUNKS:
             nc.sync.dma_start(out=planes[3][:, c0:c1], in_=x_rows[:, 3, c0:c1])
 
@@ -63,24 +63,33 @@ def tile_picked_ema_none_e_kernel(tc, xT, mem, w1, old, new, offs, slot, out):
         old_all = spread(old_col, "old_all")
         new_all = spread(new_col, "new_all")
 
-        picked = keep.tile([P, S, PACK], BF16, name="picked", align_bytes=64)
+        picked = [keep.tile([P, HALF, PACK], BF16, name=f"picked{h}", align_bytes=64) for h in range(2)]
         first = slice(0, HALF)
         second = slice(HALF, S)
         offs_first = offs_sb[:, 0 : HALF // 16]
         offs_second = offs_sb[:, HALF // 16 : S // 16]
 
-        nc.vector.tensor_copy(picked[:, first, 2], planes[2][:].indirect(offs_first))
+        nc.vector.tensor_copy(picked[0][:, :, 2], planes[2][:].indirect(offs_first))
         rounded2 = keep.tile([P, T], BF16, name="rounded2")
         nc.scalar.copy(out=rounded2[:], in_=planes[2][:])
-        nc.scalar.activation(picked[:, second, 2], rounded2[:].indirect(offs_second), COPY)
+        nc.scalar.activation(picked[1][:, :, 2], rounded2[:].indirect(offs_second), COPY)
+
+        nc.vector.tensor_copy(picked[0][:, :, 0], planes[0][:].indirect(offs_first))
+        nc.vector.tensor_copy(picked[1][:, :, 0], planes[0][:].indirect(offs_second))
 
         kept = keep.tile([P, S], F32, name="kept")
         nc.vector.tensor_tensor(kept[:], mem_sb[:].indirect(slot_sb[:]), old_all[:], MULT)
         result = keep.tile([P, U], F32, name="result")
         nc.scalar.copy(out=result[:], in_=mem_sb[:])
 
-        for j in (0, 1):
-            nc.vector.tensor_copy(picked[:, :, j], planes[j][:].indirect(offs_sb[:]))
+        nc.vector.tensor_copy(picked[1][:, :, 1], planes[1][:].indirect(offs_second))
+        nc.vector.tensor_copy(picked[0][:, :, 1], planes[1][:].indirect(offs_first))
+
+        w_grouped = keep.tile([P, N, PACK], BF16, name="w_grouped", align_bytes=64)
+        nc.scalar.copy(out=w_grouped[:], in_=w_raw[:].rearrange("p j m -> p m j"))
+        w_codes = keep.tile([P, N], U32, name="w_codes", align_bytes=64)
+        w_scales = keep.tile([P, N], U8, name="w_scales", align_bytes=64)
+        nc.vector.quantize_mx(out=w_codes[:].bitcast(FP8X4), scales=w_scales[:], in_=w_grouped[:].rearrange("p m j -> p (m j)"))
 
         rounded3 = keep.tile([P, T], BF16, name="rounded3")
         for i, (c0, c1) in enumerate(CHUNKS):
@@ -88,34 +97,35 @@ def tile_picked_ema_none_e_kernel(tc, xT, mem, w1, old, new, offs, slot, out):
                 nc.vector.tensor_copy(out=rounded3[:, c0:c1], in_=planes[3][:, c0:c1])
             else:
                 nc.scalar.copy(out=rounded3[:, c0:c1], in_=planes[3][:, c0:c1])
-        nc.vector.tensor_copy(picked[:, first, 3], planes[3][:].indirect(offs_first))
-        nc.scalar.activation(picked[:, second, 3], rounded3[:].indirect(offs_second), COPY)
+        nc.vector.tensor_copy(picked[0][:, :, 3], planes[3][:].indirect(offs_first))
+        nc.scalar.activation(picked[1][:, :, 3], rounded3[:].indirect(offs_second), COPY)
 
-        w_grouped = keep.tile([P, N, PACK], BF16, name="w_grouped", align_bytes=64)
-        nc.vector.tensor_copy(out=w_grouped[:], in_=w_raw[:].rearrange("p j m -> p m j"))
-        w_codes = keep.tile([P, N], U32, name="w_codes", align_bytes=64)
-        w_scales = keep.tile([P, N], U8, name="w_scales", align_bytes=64)
 
-        x_codes = [keep.tile([P, HALF], U32, name=f"x_codes{h}", align_bytes=64) for h in range(2)]
-        x_scales = [keep.tile([P, HALF], U8, name=f"x_scales{h}", align_bytes=64) for h in range(2)]
-        halves = (first, second)
-
-        def quantise_x(h):
-            nc.vector.quantize_mx(out=x_codes[h][:].bitcast(FP8X4), scales=x_scales[h][:], in_=picked[:, halves[h], :].rearrange("p s j -> p (s j)"))
-
-        quantise_x(0)
-        nc.vector.quantize_mx(out=w_codes[:].bitcast(FP8X4), scales=w_scales[:], in_=w_grouped[:].rearrange("p m j -> p (m j)"))
-        quantise_x(1)
+        pieces = ((0, 128), (128, 256), (256, 512))
         banks = []
-        for h in range(2):
-            y_bank = psum.tile([P, HALF], F32, name=f"y_bank{h}")
-            nc.tensor.matmul_mx(out=y_bank[:], lhsT=w_codes[:].bitcast(FP8X4), lhsT_scale=w_scales[:], rhs=x_codes[h][:].bitcast(FP8X4), rhs_scale=x_scales[h][:], start=True, stop=True)
+        for i, (s0, s1) in enumerate(pieces):
+            h, o = divmod(s0, HALF)
+            width = s1 - s0
+            x_codes = keep.tile([P, width], U32, name=f"x_codes{i}", align_bytes=64)
+            x_scales = keep.tile([P, width], U8, name=f"x_scales{i}", align_bytes=64)
+            nc.vector.quantize_mx(out=x_codes[:].bitcast(FP8X4), scales=x_scales[:], in_=picked[h][:, o : o + width, :].rearrange("p s j -> p (s j)"))
+            y_bank = psum.tile([P, width], F32, name=f"y_bank{i}")
+            nc.tensor.matmul_mx(out=y_bank[:], lhsT=w_codes[:].bitcast(FP8X4), lhsT_scale=w_scales[:], rhs=x_codes[:].bitcast(FP8X4), rhs_scale=x_scales[:], start=True, stop=True)
             banks.append(y_bank)
-        added = []
-        for h in range(2):
-            y_new = keep.tile([P, HALF], F32, name=f"y_new{h}")
-            nc.vector.tensor_tensor(y_new[:], banks[h][:], new_all[:, halves[h]], MULT)
-            added.append(y_new)
-        for h in range(2):
-            nc.vector.tensor_tensor(result[:].indirect(slot_sb[:, h * HALF // 16 : (h + 1) * HALF // 16]), kept[:, halves[h]], added[h][:], ADD)
+        added = [keep.tile([P, s1 - s0], F32, name=f"y_new{i}") for i, (s0, s1) in enumerate(pieces)]
+
+        def weigh(i):
+            s0, s1 = pieces[i]
+            nc.vector.tensor_tensor(added[i][:], banks[i][:], new_all[:, s0:s1], MULT)
+
+        def put(i):
+            s0, s1 = pieces[i]
+            nc.vector.tensor_tensor(result[:].indirect(slot_sb[:, s0 // 16 : s1 // 16]), kept[:, s0:s1], added[i][:], ADD)
+
+        weigh(0)
+        weigh(1)
+        put(0)
+        weigh(2)
+        put(1)
+        put(2)
         nc.sync.dma_start(out=out, in_=result[:])

@@ -19,7 +19,7 @@ ADD = mybir.AluOpType.add
 COPY = mybir.ActivationFunctionType.Copy
 
 HALF = S // 2
-CHUNKS = ((0, 1024), (1024, 1536), (1536, 1792), (1792, 2048))
+CHUNKS = ((0, 1024), (1024, 1536), (1536, 2048))
 
 
 def tile_picked_ema_none_e_kernel(tc, xT, mem, w1, old, new, offs, slot, out):
@@ -41,13 +41,15 @@ def tile_picked_ema_none_e_kernel(tc, xT, mem, w1, old, new, offs, slot, out):
         slot_sb = keep.tile([P, S // 16], U16, name="slot_sb")
         nc.sync.dma_start(slot_sb[:], slot)
         nc.sync.dma_start(out=planes[0][:], in_=x_rows[:, 0, :])
-        mem_sb = keep.tile([P, U], F32, name="mem_sb")
-        nc.sync.dma_start(out=mem_sb[:], in_=mem)
         nc.sync.dma_start(out=planes[1][:], in_=x_rows[:, 1, :])
-        w_raw = keep.tile([P, PACK, N], F32, name="w_raw")
-        nc.sync.dma_start(out=w_raw[:], in_=w1.rearrange("(p j) m -> p j m", j=PACK))
         for c0, c1 in CHUNKS:
             nc.sync.dma_start(out=planes[3][:, c0:c1], in_=x_rows[:, 3, c0:c1])
+        w_raw = keep.tile([P, PACK, N], F32, name="w_raw")
+        nc.sync.dma_start(out=w_raw[:], in_=w1.rearrange("(p j) m -> p j m", j=PACK))
+        mem_sb = keep.tile([P, U], F32, name="mem_sb")
+        nc.sync.dma_start(out=mem_sb[:], in_=mem)
+        result = keep.tile([P, U], F32, name="result")
+        nc.sync.dma_start(out=result[:], in_=mem)
 
         ident = keep.tile([P, P], F32, name="ident")
         make_identity(nc, ident[:])
@@ -77,55 +79,54 @@ def tile_picked_ema_none_e_kernel(tc, xT, mem, w1, old, new, offs, slot, out):
         nc.vector.tensor_copy(picked[0][:, :, 0], planes[0][:].indirect(offs_first))
         nc.vector.tensor_copy(picked[1][:, :, 0], planes[0][:].indirect(offs_second))
 
-        kept = keep.tile([P, S], F32, name="kept")
-        nc.vector.tensor_tensor(kept[:], mem_sb[:].indirect(slot_sb[:]), old_all[:], MULT)
-        result = keep.tile([P, U], F32, name="result")
-        nc.scalar.copy(out=result[:], in_=mem_sb[:])
-
         nc.vector.tensor_copy(picked[1][:, :, 1], planes[1][:].indirect(offs_second))
         nc.vector.tensor_copy(picked[0][:, :, 1], planes[1][:].indirect(offs_first))
 
+        rounded3 = keep.tile([P, T], BF16, name="rounded3")
+        for c0, c1 in CHUNKS[:-1]:
+            nc.vector.tensor_copy(out=rounded3[:, c0:c1], in_=planes[3][:, c0:c1])
+        c0, c1 = CHUNKS[-1]
+        nc.scalar.copy(out=rounded3[:, c0:c1], in_=planes[3][:, c0:c1])
+        nc.vector.tensor_copy(picked[0][:, :, 3], planes[3][:].indirect(offs_first))
         w_grouped = keep.tile([P, N, PACK], BF16, name="w_grouped", align_bytes=64)
         nc.scalar.copy(out=w_grouped[:], in_=w_raw[:].rearrange("p j m -> p m j"))
-        w_codes = keep.tile([P, N], U32, name="w_codes", align_bytes=64)
-        w_scales = keep.tile([P, N], U8, name="w_scales", align_bytes=64)
-        nc.vector.quantize_mx(out=w_codes[:].bitcast(FP8X4), scales=w_scales[:], in_=w_grouped[:].rearrange("p m j -> p (m j)"))
-
-        rounded3 = keep.tile([P, T], BF16, name="rounded3")
-        for i, (c0, c1) in enumerate(CHUNKS):
-            if i > 0:
-                nc.vector.tensor_copy(out=rounded3[:, c0:c1], in_=planes[3][:, c0:c1])
-            else:
-                nc.scalar.copy(out=rounded3[:, c0:c1], in_=planes[3][:, c0:c1])
-        nc.vector.tensor_copy(picked[0][:, :, 3], planes[3][:].indirect(offs_first))
         nc.scalar.activation(picked[1][:, :, 3], rounded3[:].indirect(offs_second), COPY)
 
+        halves = (first, second)
+        slots = (slot_sb[:, 0 : HALF // 16], slot_sb[:, HALF // 16 : S // 16])
+        w_codes = keep.tile([P, N], U32, name="w_codes", align_bytes=64)
+        w_scales = keep.tile([P, N], U8, name="w_scales", align_bytes=64)
+        codes, scales, banks, kept, added = {}, {}, {}, {}, {}
 
-        pieces = ((0, 128), (128, 256), (256, 512))
-        banks = []
-        for i, (s0, s1) in enumerate(pieces):
-            h, o = divmod(s0, HALF)
-            width = s1 - s0
-            x_codes = keep.tile([P, width], U32, name=f"x_codes{i}", align_bytes=64)
-            x_scales = keep.tile([P, width], U8, name=f"x_scales{i}", align_bytes=64)
-            nc.vector.quantize_mx(out=x_codes[:].bitcast(FP8X4), scales=x_scales[:], in_=picked[h][:, o : o + width, :].rearrange("p s j -> p (s j)"))
-            y_bank = psum.tile([P, width], F32, name=f"y_bank{i}")
-            nc.tensor.matmul_mx(out=y_bank[:], lhsT=w_codes[:].bitcast(FP8X4), lhsT_scale=w_scales[:], rhs=x_codes[:].bitcast(FP8X4), rhs_scale=x_scales[:], start=True, stop=True)
-            banks.append(y_bank)
-        added = [keep.tile([P, s1 - s0], F32, name=f"y_new{i}") for i, (s0, s1) in enumerate(pieces)]
+        def quantise(h):
+            codes[h] = keep.tile([P, HALF], U32, name=f"x_codes{h}", align_bytes=64)
+            scales[h] = keep.tile([P, HALF], U8, name=f"x_scales{h}", align_bytes=64)
+            nc.vector.quantize_mx(out=codes[h][:].bitcast(FP8X4), scales=scales[h][:], in_=picked[h][:].rearrange("p s j -> p (s j)"))
 
-        def weigh(i):
-            s0, s1 = pieces[i]
-            nc.vector.tensor_tensor(added[i][:], banks[i][:], new_all[:, s0:s1], MULT)
+        def project(h):
+            banks[h] = psum.tile([P, HALF], F32, name=f"y_bank{h}")
+            nc.tensor.matmul_mx(out=banks[h][:], lhsT=w_codes[:].bitcast(FP8X4), lhsT_scale=w_scales[:], rhs=codes[h][:].bitcast(FP8X4), rhs_scale=scales[h][:], start=True, stop=True)
 
-        def put(i):
-            s0, s1 = pieces[i]
-            nc.vector.tensor_tensor(result[:].indirect(slot_sb[:, s0 // 16 : s1 // 16]), kept[:, s0:s1], added[i][:], ADD)
+        def fetch(h, tag):
+            kept[h] = keep.tile([P, HALF], F32, name=f"kept{h}", tag=tag, align_bytes=64)
+            nc.vector.tensor_tensor(kept[h][:], mem_sb[:].indirect(slots[h]), old_all[:, halves[h]], MULT)
 
+        def weigh(h):
+            added[h] = keep.tile([P, HALF], F32, name=f"y_new{h}")
+            nc.vector.tensor_tensor(added[h][:], banks[h][:], new_all[:, halves[h]], MULT)
+
+        def put(h):
+            nc.vector.tensor_tensor(result[:].indirect(slots[h]), kept[h][:], added[h][:], ADD)
+
+        quantise(0)
+        nc.vector.quantize_mx(out=w_codes[:].bitcast(FP8X4), scales=w_scales[:], in_=w_grouped[:].rearrange("p m j -> p (m j)"))
+        project(0)
+        fetch(0, "kept0")
         weigh(0)
-        weigh(1)
+        quantise(1)
+        project(1)
         put(0)
-        weigh(2)
+        fetch(1, "x_codes0")
+        weigh(1)
         put(1)
-        put(2)
         nc.sync.dma_start(out=out, in_=result[:])

@@ -19,6 +19,7 @@ ADD = mybir.AluOpType.add
 COPY = mybir.ActivationFunctionType.Copy
 
 HALF = S // 2
+GROUPS = S // P
 CHUNKS = ((0, 1024), (1024, 1536), (1536, 2048))
 
 
@@ -31,10 +32,10 @@ def tile_picked_ema_none_e_kernel(tc, xT, mem, w1, old, new, offs, slot, out):
         x_rows = xT.rearrange("(p j) t -> p j t", j=PACK)
         planes = [keep.tile([P, T], F32, name=f"plane{j}") for j in range(PACK)]
 
-        old_col = keep.tile([P, PACK], F32, name="old_col")
-        nc.scalar.dma_start(out=old_col[:], in_=old[0:1, :].rearrange("o (p c) -> (o p) c", c=PACK))
-        new_col = keep.tile([P, PACK], F32, name="new_col")
-        nc.scalar.dma_start(out=new_col[:], in_=new[0:1, :].rearrange("o (p c) -> (o p) c", c=PACK))
+        flat = keep.tile([P, P], F32, name="flat")
+        nc.gpsimd.memset(flat[:], 0.0)
+        nc.scalar.dma_start(out=flat[0:GROUPS, :], in_=old[0:1, :].rearrange("o (c p) -> (o c) p", p=P))
+        nc.scalar.dma_start(out=flat[GROUPS : 2 * GROUPS, :], in_=new[0:1, :].rearrange("o (c p) -> (o c) p", p=P))
         offs_sb = keep.tile([P, S // 16], U16, name="offs_sb")
         nc.sync.dma_start(out=planes[2][:], in_=x_rows[:, 2, :])
         nc.sync.dma_start(offs_sb[:], offs)
@@ -54,16 +55,21 @@ def tile_picked_ema_none_e_kernel(tc, xT, mem, w1, old, new, offs, slot, out):
         ident = keep.tile([P, P], F32, name="ident")
         make_identity(nc, ident[:])
 
-        def spread(col, name):
-            bank = psum.tile([P, PACK, P], F32, name=name + "_bank")
-            for c in range(PACK):
-                nc.tensor.transpose(bank[:, c, :], col[:, c : c + 1].to_broadcast([P, P]), ident[:])
-            full = keep.tile([P, S], F32, name=name)
-            nc.scalar.copy(out=full[:].rearrange("p (k c) -> p k c", c=PACK), in_=bank[:].rearrange("p c k -> p k c"))
+        turn_bank = psum.tile([P, P], F32, name="turn_bank")
+        nc.tensor.transpose(turn_bank[:], flat[:], ident[:])
+        by_row = keep.tile([P, 2 * GROUPS], F32, name="by_row")
+        nc.scalar.copy(out=by_row[:], in_=turn_bank[:, 0 : 2 * GROUPS])
+
+        def spread(start, groups, name):
+            bank = psum.tile([P, groups, P], F32, name=name + "_bank")
+            for c in range(groups):
+                nc.tensor.transpose(bank[:, c, :], by_row[:, start + c : start + c + 1].to_broadcast([P, P]), ident[:])
+            full = keep.tile([P, groups * P], F32, name=name)
+            nc.scalar.copy(out=full[:], in_=bank[:].rearrange("p c k -> p (c k)"))
             return full
 
-        old_all = spread(old_col, "old_all")
-        new_all = spread(new_col, "new_all")
+        old_all = spread(0, GROUPS, "old_all")
+        new_all = spread(GROUPS, 2, "new_all")
 
         picked = [keep.tile([P, HALF, PACK], BF16, name=f"picked{h}", align_bytes=64) for h in range(2)]
         first = slice(0, HALF)
@@ -83,10 +89,11 @@ def tile_picked_ema_none_e_kernel(tc, xT, mem, w1, old, new, offs, slot, out):
         nc.vector.tensor_copy(picked[0][:, :, 1], planes[1][:].indirect(offs_first))
 
         rounded3 = keep.tile([P, T], BF16, name="rounded3")
-        for c0, c1 in CHUNKS[:-1]:
-            nc.vector.tensor_copy(out=rounded3[:, c0:c1], in_=planes[3][:, c0:c1])
-        c0, c1 = CHUNKS[-1]
-        nc.scalar.copy(out=rounded3[:, c0:c1], in_=planes[3][:, c0:c1])
+        for i, (c0, c1) in enumerate(CHUNKS):
+            if i == 1:
+                nc.vector.tensor_copy(out=rounded3[:, c0:c1], in_=planes[3][:, c0:c1])
+            else:
+                nc.scalar.copy(out=rounded3[:, c0:c1], in_=planes[3][:, c0:c1])
         nc.vector.tensor_copy(picked[0][:, :, 3], planes[3][:].indirect(offs_first))
         w_grouped = keep.tile([P, N, PACK], BF16, name="w_grouped", align_bytes=64)
         nc.scalar.copy(out=w_grouped[:], in_=w_raw[:].rearrange("p j m -> p m j"))
@@ -124,9 +131,19 @@ def tile_picked_ema_none_e_kernel(tc, xT, mem, w1, old, new, offs, slot, out):
         fetch(0, "kept0")
         weigh(0)
         quantise(1)
-        project(1)
-        put(0)
+        rows_bank = psum.tile([P, 2, N], F32, name="rows_bank")
+        rows = keep.tile([P, 2, N], F32, name="rows")
+        back_bank = psum.tile([P, 2, P], F32, name="back_bank")
+        for c in range(2):
+            cols = slice(c * P, (c + 1) * P)
+            nc.tensor.matmul_mx(out=rows_bank[:, c, :], lhsT=codes[1][:, cols].bitcast(FP8X4), lhsT_scale=scales[1][:, cols], rhs=w_codes[:].bitcast(FP8X4), rhs_scale=w_scales[:], start=True, stop=True)
+        for c in range(2):
+            nc.scalar.activation(rows[:, c, :], rows_bank[:, c, :], COPY, scale=by_row[:, GROUPS + 2 + c : GROUPS + 3 + c])
+        for c in range(2):
+            nc.tensor.transpose(back_bank[:, c, :], rows[:, c, :], ident[:])
+        added[1] = keep.tile([P, HALF], F32, name="y_new1")
+        nc.scalar.copy(out=added[1][:], in_=back_bank[:].rearrange("p c k -> p (c k)"))
         fetch(1, "x_codes0")
-        weigh(1)
+        put(0)
         put(1)
         nc.sync.dma_start(out=out, in_=result[:])

@@ -30,7 +30,7 @@ def tile_picked_ema_none_e_kernel(tc, xT, mem, w1, old, new, offs, slot, out):
         psum = ctx.enter_context(tc.psum_pool(name="psum", bufs=1))
 
         x_rows = xT.rearrange("(p j) t -> p j t", j=PACK)
-        planes = [keep.tile([P, T], F32, name=f"plane{j}") for j in range(PACK)]
+        planes = [keep.tile([P, T], F32, name=f"plane{j}", align_bytes=64) for j in range(PACK)]
 
         flat = keep.tile([P, P], F32, name="flat")
         nc.gpsimd.memset(flat[:], 0.0)
@@ -96,7 +96,7 @@ def tile_picked_ema_none_e_kernel(tc, xT, mem, w1, old, new, offs, slot, out):
                 nc.scalar.copy(out=rounded3[:, c0:c1], in_=planes[3][:, c0:c1])
         nc.vector.tensor_copy(picked[0][:, :, 3], planes[3][:].indirect(offs_first))
         w_grouped = keep.tile([P, N, PACK], BF16, name="w_grouped", align_bytes=64)
-        nc.scalar.copy(out=w_grouped[:], in_=w_raw[:].rearrange("p j m -> p m j"))
+        nc.vector.tensor_copy(out=w_grouped[:].rearrange("p (c i) j -> p c j i", i=4), in_=w_raw[:].rearrange("p j (c i) -> p c j i", i=4))
         nc.scalar.activation(picked[1][:, :, 3], rounded3[:].indirect(offs_second), COPY)
 
         halves = (first, second)
@@ -105,8 +105,8 @@ def tile_picked_ema_none_e_kernel(tc, xT, mem, w1, old, new, offs, slot, out):
         w_scales = keep.tile([P, N], U8, name="w_scales", align_bytes=64)
         codes, scales, banks, kept, added = {}, {}, {}, {}, {}
 
-        def quantise(h):
-            codes[h] = keep.tile([P, HALF], U32, name=f"x_codes{h}", align_bytes=64)
+        def quantise(h, tag):
+            codes[h] = keep.tile([P, HALF], U32, name=f"x_codes{h}", tag=tag, align_bytes=64)
             scales[h] = keep.tile([P, HALF], U8, name=f"x_scales{h}", align_bytes=64)
             nc.vector.quantize_mx(out=codes[h][:].bitcast(FP8X4), scales=scales[h][:], in_=picked[h][:].rearrange("p s j -> p (s j)"))
 
@@ -125,12 +125,12 @@ def tile_picked_ema_none_e_kernel(tc, xT, mem, w1, old, new, offs, slot, out):
         def put(h):
             nc.vector.tensor_tensor(result[:].indirect(slots[h]), kept[h][:], added[h][:], ADD)
 
-        quantise(0)
+        quantise(0, "plane3")
         nc.vector.quantize_mx(out=w_codes[:].bitcast(FP8X4), scales=w_scales[:], in_=w_grouped[:].rearrange("p m j -> p (m j)"))
         project(0)
+        quantise(1, "x_codes1")
         fetch(0, "kept0")
         weigh(0)
-        quantise(1)
         rows_bank = psum.tile([P, 2, N], F32, name="rows_bank")
         rows = keep.tile([P, 2, N], F32, name="rows")
         back_bank = psum.tile([P, 2, P], F32, name="back_bank")
@@ -143,7 +143,7 @@ def tile_picked_ema_none_e_kernel(tc, xT, mem, w1, old, new, offs, slot, out):
             nc.tensor.transpose(back_bank[:, c, :], rows[:, c, :], ident[:])
         added[1] = keep.tile([P, HALF], F32, name="y_new1")
         nc.scalar.copy(out=added[1][:], in_=back_bank[:].rearrange("p c k -> p (c k)"))
-        fetch(1, "x_codes0")
+        fetch(1, "plane3")
         put(0)
         put(1)
         nc.sync.dma_start(out=out, in_=result[:])

@@ -34,19 +34,19 @@ def tile_picked_ema_none_e_kernel(tc, xT, mem, w1, old, new, offs, slot, out):
 
         flat = keep.tile([P, P], F32, name="flat")
         nc.gpsimd.memset(flat[:], 0.0)
-        nc.scalar.dma_start(out=flat[0:GROUPS, :], in_=old[0:1, :].rearrange("o (c p) -> (o c) p", p=P))
-        nc.scalar.dma_start(out=flat[GROUPS : 2 * GROUPS, :], in_=new[0:1, :].rearrange("o (c p) -> (o c) p", p=P))
         offs_sb = keep.tile([P, S // 16], U16, name="offs_sb")
         nc.sync.dma_start(out=planes[2][:], in_=x_rows[:, 2, :])
         nc.sync.dma_start(offs_sb[:], offs)
-        slot_sb = keep.tile([P, S // 16], U16, name="slot_sb")
-        nc.sync.dma_start(slot_sb[:], slot)
+        nc.sync.dma_start(out=flat[0:GROUPS, :], in_=old[0:1, :].rearrange("o (c p) -> (o c) p", p=P))
+        nc.sync.dma_start(out=flat[GROUPS : 2 * GROUPS, :], in_=new[0:1, :].rearrange("o (c p) -> (o c) p", p=P))
         nc.sync.dma_start(out=planes[0][:], in_=x_rows[:, 0, :])
         nc.sync.dma_start(out=planes[1][:], in_=x_rows[:, 1, :])
         for c0, c1 in CHUNKS:
             nc.sync.dma_start(out=planes[3][:, c0:c1], in_=x_rows[:, 3, c0:c1])
         w_raw = keep.tile([P, PACK, N], F32, name="w_raw")
         nc.sync.dma_start(out=w_raw[:], in_=w1.rearrange("(p j) m -> p j m", j=PACK))
+        slot_sb = keep.tile([P, S // 16], U16, name="slot_sb")
+        nc.sync.dma_start(slot_sb[:], slot)
         mem_sb = keep.tile([P, U], F32, name="mem_sb")
         nc.sync.dma_start(out=mem_sb[:], in_=mem)
         result = keep.tile([P, U], F32, name="result")

@@ -20,7 +20,8 @@ COPY = mybir.ActivationFunctionType.Copy
 
 HALF = S // 2
 GROUPS = S // P
-CHUNKS = ((0, 1024), (1024, 1536), (1536, 2048))
+CHUNKS = ((0, 1536), (1536, 2048))
+ROUNDING = ((0, 512), (512, 1536), (1536, 2048))
 
 
 def tile_picked_ema_none_e_kernel(tc, xT, mem, w1, old, new, offs, slot, out):
@@ -69,11 +70,9 @@ def tile_picked_ema_none_e_kernel(tc, xT, mem, w1, old, new, offs, slot, out):
             return full
 
         old_all = spread(0, GROUPS, "old_all")
-        new_all = spread(GROUPS, 2, "new_all")
+        new_all = spread(GROUPS, 1, "new_all")
 
         picked = [keep.tile([P, HALF, PACK], BF16, name=f"picked{h}", align_bytes=64) for h in range(2)]
-        first = slice(0, HALF)
-        second = slice(HALF, S)
         offs_first = offs_sb[:, 0 : HALF // 16]
         offs_second = offs_sb[:, HALF // 16 : S // 16]
 
@@ -89,7 +88,7 @@ def tile_picked_ema_none_e_kernel(tc, xT, mem, w1, old, new, offs, slot, out):
         nc.vector.tensor_copy(picked[0][:, :, 1], planes[1][:].indirect(offs_first))
 
         rounded3 = keep.tile([P, T], BF16, name="rounded3")
-        for i, (c0, c1) in enumerate(CHUNKS):
+        for i, (c0, c1) in enumerate(ROUNDING):
             if i == 1:
                 nc.vector.tensor_copy(out=rounded3[:, c0:c1], in_=planes[3][:, c0:c1])
             else:
@@ -99,51 +98,48 @@ def tile_picked_ema_none_e_kernel(tc, xT, mem, w1, old, new, offs, slot, out):
         nc.vector.tensor_copy(out=w_grouped[:].rearrange("p (c i) j -> p c j i", i=4), in_=w_raw[:].rearrange("p j (c i) -> p c j i", i=4))
         nc.scalar.activation(picked[1][:, :, 3], rounded3[:].indirect(offs_second), COPY)
 
-        halves = (first, second)
-        slots = (slot_sb[:, 0 : HALF // 16], slot_sb[:, HALF // 16 : S // 16])
         w_codes = keep.tile([P, N], U32, name="w_codes", align_bytes=64)
         w_scales = keep.tile([P, N], U8, name="w_scales", align_bytes=64)
-        codes, scales, banks, kept, added = {}, {}, {}, {}, {}
+        codes, scales = {}, {}
 
         def quantise(h, tag):
             codes[h] = keep.tile([P, HALF], U32, name=f"x_codes{h}", tag=tag, align_bytes=64)
             scales[h] = keep.tile([P, HALF], U8, name=f"x_scales{h}", align_bytes=64)
             nc.vector.quantize_mx(out=codes[h][:].bitcast(FP8X4), scales=scales[h][:], in_=picked[h][:].rearrange("p s j -> p (s j)"))
 
-        def project(h):
-            banks[h] = psum.tile([P, HALF], F32, name=f"y_bank{h}")
-            nc.tensor.matmul_mx(out=banks[h][:], lhsT=w_codes[:].bitcast(FP8X4), lhsT_scale=w_scales[:], rhs=codes[h][:].bitcast(FP8X4), rhs_scale=scales[h][:], start=True, stop=True)
+        def slots(entries):
+            return slot_sb[:, entries.start // 16 : entries.stop // 16]
 
-        def fetch(h, tag):
-            kept[h] = keep.tile([P, HALF], F32, name=f"kept{h}", tag=tag, align_bytes=64)
-            nc.vector.tensor_tensor(kept[h][:], mem_sb[:].indirect(slots[h]), old_all[:, halves[h]], MULT)
-
-        def weigh(h):
-            added[h] = keep.tile([P, HALF], F32, name=f"y_new{h}")
-            nc.vector.tensor_tensor(added[h][:], banks[h][:], new_all[:, halves[h]], MULT)
-
-        def put(h):
-            nc.vector.tensor_tensor(result[:].indirect(slots[h]), kept[h][:], added[h][:], ADD)
-
+        early = slice(0, P)
+        late = slice(P, S)
         quantise(0, "plane3")
         nc.vector.quantize_mx(out=w_codes[:].bitcast(FP8X4), scales=w_scales[:], in_=w_grouped[:].rearrange("p m j -> p (m j)"))
-        project(0)
+        y_bank = psum.tile([P, P], F32, name="y_bank")
+        nc.tensor.matmul_mx(out=y_bank[:], lhsT=w_codes[:].bitcast(FP8X4), lhsT_scale=w_scales[:], rhs=codes[0][:, 0:P].bitcast(FP8X4), rhs_scale=scales[0][:, 0:P], start=True, stop=True)
+        rows = keep.tile([P, GROUPS - 1, N], F32, name="rows")
+        added_late = keep.tile([P, S - P], F32, name="added_late")
+
+        def through_scalar(groups, name):
+            bank = psum.tile([P, len(groups), N], F32, name=name)
+            for i, g in enumerate(groups):
+                cols = slice(g % 2 * P, (g % 2 + 1) * P)
+                nc.tensor.matmul_mx(out=bank[:, i, :], lhsT=codes[g // 2][:, cols].bitcast(FP8X4), lhsT_scale=scales[g // 2][:, cols], rhs=w_codes[:].bitcast(FP8X4), rhs_scale=w_scales[:], start=True, stop=True)
+            for i, g in enumerate(groups):
+                nc.scalar.activation(rows[:, g - 1, :], bank[:, i, :], COPY, scale=by_row[:, GROUPS + g : GROUPS + g + 1])
+            back = psum.tile([P, len(groups), P], F32, name=name + "_back")
+            for i, g in enumerate(groups):
+                nc.tensor.transpose(back[:, i, :], rows[:, g - 1, :], ident[:])
+            nc.scalar.copy(out=added_late[:, (groups[0] - 1) * P : groups[-1] * P], in_=back[:].rearrange("p c k -> p (c k)"))
+
+        through_scalar([1], "rows_bank0")
         quantise(1, "x_codes1")
-        fetch(0, "kept0")
-        weigh(0)
-        rows_bank = psum.tile([P, 2, N], F32, name="rows_bank")
-        rows = keep.tile([P, 2, N], F32, name="rows")
-        back_bank = psum.tile([P, 2, P], F32, name="back_bank")
-        for c in range(2):
-            cols = slice(c * P, (c + 1) * P)
-            nc.tensor.matmul_mx(out=rows_bank[:, c, :], lhsT=codes[1][:, cols].bitcast(FP8X4), lhsT_scale=scales[1][:, cols], rhs=w_codes[:].bitcast(FP8X4), rhs_scale=w_scales[:], start=True, stop=True)
-        for c in range(2):
-            nc.scalar.activation(rows[:, c, :], rows_bank[:, c, :], COPY, scale=by_row[:, GROUPS + 2 + c : GROUPS + 3 + c])
-        for c in range(2):
-            nc.tensor.transpose(back_bank[:, c, :], rows[:, c, :], ident[:])
-        added[1] = keep.tile([P, HALF], F32, name="y_new1")
-        nc.scalar.copy(out=added[1][:], in_=back_bank[:].rearrange("p c k -> p (c k)"))
-        fetch(1, "plane3")
-        put(0)
-        put(1)
+        kept_early = keep.tile([P, P], F32, name="kept_early")
+        nc.vector.tensor_tensor(kept_early[:], mem_sb[:].indirect(slots(early)), old_all[:, early], MULT)
+        added_early = keep.tile([P, P], F32, name="added_early")
+        nc.vector.tensor_tensor(added_early[:], y_bank[:], new_all[:], MULT)
+        through_scalar([2, 3], "rows_bank1")
+        kept_late = keep.tile([P, S - P], F32, name="kept_late", tag="plane3", align_bytes=64)
+        nc.vector.tensor_tensor(kept_late[:], mem_sb[:].indirect(slots(late)), old_all[:, late], MULT)
+        nc.vector.tensor_tensor(result[:].indirect(slots(early)), kept_early[:], added_early[:], ADD)
+        nc.vector.tensor_tensor(result[:].indirect(slots(late)), kept_late[:], added_late[:], ADD)
         nc.sync.dma_start(out=out, in_=result[:])

@@ -102,42 +102,44 @@ def tile_picked_ema_none_e_kernel(tc, xT, mem, w1, old, new, offs, slot, out):
         w_scales = keep.tile([P, N], U8, name="w_scales", align_bytes=64)
         codes, scales = {}, {}
 
-        def quantise(h, tag):
+        def quantise(h, tag, pieces):
             codes[h] = keep.tile([P, HALF], U32, name=f"x_codes{h}", tag=tag, align_bytes=64)
             scales[h] = keep.tile([P, HALF], U8, name=f"x_scales{h}", align_bytes=64)
-            nc.vector.quantize_mx(out=codes[h][:].bitcast(FP8X4), scales=scales[h][:], in_=picked[h][:].rearrange("p s j -> p (s j)"))
+            for cols in pieces:
+                nc.vector.quantize_mx(out=codes[h][:, cols].bitcast(FP8X4), scales=scales[h][:, cols], in_=picked[h][:, cols, :].rearrange("p s j -> p (s j)"))
 
         def slots(entries):
             return slot_sb[:, entries.start // 16 : entries.stop // 16]
 
         early = slice(0, P)
         late = slice(P, S)
-        quantise(0, "plane3")
+        quantise(0, "plane3", [slice(0, HALF)])
         nc.vector.quantize_mx(out=w_codes[:].bitcast(FP8X4), scales=w_scales[:], in_=w_grouped[:].rearrange("p m j -> p (m j)"))
         y_bank = psum.tile([P, P], F32, name="y_bank")
         nc.tensor.matmul_mx(out=y_bank[:], lhsT=w_codes[:].bitcast(FP8X4), lhsT_scale=w_scales[:], rhs=codes[0][:, 0:P].bitcast(FP8X4), rhs_scale=scales[0][:, 0:P], start=True, stop=True)
         rows = keep.tile([P, GROUPS - 1, N], F32, name="rows")
         added_late = keep.tile([P, S - P], F32, name="added_late")
 
-        def through_scalar(groups, name):
-            bank = psum.tile([P, len(groups), N], F32, name=name)
+        def through_scalar(groups, name, tag, back_tag):
+            bank = psum.tile([P, len(groups), N], F32, name=name, tag=tag)
             for i, g in enumerate(groups):
                 cols = slice(g % 2 * P, (g % 2 + 1) * P)
                 nc.tensor.matmul_mx(out=bank[:, i, :], lhsT=codes[g // 2][:, cols].bitcast(FP8X4), lhsT_scale=scales[g // 2][:, cols], rhs=w_codes[:].bitcast(FP8X4), rhs_scale=w_scales[:], start=True, stop=True)
             for i, g in enumerate(groups):
                 nc.scalar.activation(rows[:, g - 1, :], bank[:, i, :], COPY, scale=by_row[:, GROUPS + g : GROUPS + g + 1])
-            back = psum.tile([P, len(groups), P], F32, name=name + "_back")
+            back = psum.tile([P, len(groups), P], F32, name=name + "_back", tag=back_tag)
             for i, g in enumerate(groups):
                 nc.tensor.transpose(back[:, i, :], rows[:, g - 1, :], ident[:])
             nc.scalar.copy(out=added_late[:, (groups[0] - 1) * P : groups[-1] * P], in_=back[:].rearrange("p c k -> p (c k)"))
 
-        through_scalar([1], "rows_bank0")
-        quantise(1, "x_codes1")
+        through_scalar([1], "rows_bank1", "turn_bank", "old_all_bank")
+        quantise(1, "x_codes1", [slice(0, P), slice(P, HALF)])
         kept_early = keep.tile([P, P], F32, name="kept_early")
         nc.vector.tensor_tensor(kept_early[:], mem_sb[:].indirect(slots(early)), old_all[:, early], MULT)
         added_early = keep.tile([P, P], F32, name="added_early")
         nc.vector.tensor_tensor(added_early[:], y_bank[:], new_all[:], MULT)
-        through_scalar([2, 3], "rows_bank1")
+        through_scalar([2], "rows_bank2", "rows_bank2", "back_bank2")
+        through_scalar([3], "rows_bank3", "rows_bank3", "back_bank3")
         kept_late = keep.tile([P, S - P], F32, name="kept_late", tag="plane3", align_bytes=64)
         nc.vector.tensor_tensor(kept_late[:], mem_sb[:].indirect(slots(late)), old_all[:, late], MULT)
         nc.vector.tensor_tensor(result[:].indirect(slots(early)), kept_early[:], added_early[:], ADD)

@@ -20,8 +20,8 @@ COPY = mybir.ActivationFunctionType.Copy
 
 HALF = S // 2
 GROUPS = S // P
-CHUNKS = ((0, 1536), (1536, 2048))
-ROUNDING = ((0, 512), (512, 1536), (1536, 2048))
+COPIED = 512
+CHUNKS = ((0, 1024), (1024, 1536), (1536, 2048))
 
 
 def tile_picked_ema_none_e_kernel(tc, xT, mem, w1, old, new, offs, slot, out):
@@ -46,12 +46,13 @@ def tile_picked_ema_none_e_kernel(tc, xT, mem, w1, old, new, offs, slot, out):
             nc.sync.dma_start(out=planes[3][:, c0:c1], in_=x_rows[:, 3, c0:c1])
         w_raw = keep.tile([P, PACK, N], F32, name="w_raw")
         nc.sync.dma_start(out=w_raw[:], in_=w1.rearrange("(p j) m -> p j m", j=PACK))
+        mem_sb = keep.tile([P, U], F32, name="mem_sb")
+        nc.sync.dma_start(out=mem_sb[:, 0:COPIED], in_=mem[:, 0:COPIED])
+        nc.sync.dma_start(out=mem_sb[:, COPIED:], in_=mem[:, COPIED:])
         slot_sb = keep.tile([P, S // 16], U16, name="slot_sb")
         nc.sync.dma_start(slot_sb[:], slot)
-        mem_sb = keep.tile([P, U], F32, name="mem_sb")
-        nc.sync.dma_start(out=mem_sb[:], in_=mem)
         result = keep.tile([P, U], F32, name="result")
-        nc.sync.dma_start(out=result[:], in_=mem)
+        nc.sync.dma_start(out=result[:, COPIED:], in_=mem[:, COPIED:])
 
         ident = keep.tile([P, P], F32, name="ident")
         make_identity(nc, ident[:])
@@ -88,7 +89,7 @@ def tile_picked_ema_none_e_kernel(tc, xT, mem, w1, old, new, offs, slot, out):
         nc.vector.tensor_copy(picked[0][:, :, 1], planes[1][:].indirect(offs_first))
 
         rounded3 = keep.tile([P, T], BF16, name="rounded3")
-        for i, (c0, c1) in enumerate(ROUNDING):
+        for i, (c0, c1) in enumerate(CHUNKS):
             if i == 1:
                 nc.vector.tensor_copy(out=rounded3[:, c0:c1], in_=planes[3][:, c0:c1])
             else:
@@ -98,6 +99,7 @@ def tile_picked_ema_none_e_kernel(tc, xT, mem, w1, old, new, offs, slot, out):
         nc.vector.tensor_copy(out=w_grouped[:].rearrange("p (c i) j -> p c j i", i=4), in_=w_raw[:].rearrange("p j (c i) -> p c j i", i=4))
         nc.scalar.activation(picked[1][:, :, 3], rounded3[:].indirect(offs_second), COPY)
 
+        nc.scalar.copy(out=result[:, 0:COPIED], in_=mem_sb[:, 0:COPIED])
         w_codes = keep.tile([P, N], U32, name="w_codes", align_bytes=64)
         w_scales = keep.tile([P, N], U8, name="w_scales", align_bytes=64)
         codes, scales = {}, {}

@@ -21,7 +21,8 @@ COPY = mybir.ActivationFunctionType.Copy
 HALF = S // 2
 GROUPS = S // P
 COPIED = 512
-CHUNKS = ((0, 1024), (1024, 1536), (1536, 2048))
+CHUNKS = ((0, 1536), (1536, 2048))
+ROUNDING = ((0, 512), (512, 1536), (1536, 2048))
 
 
 def tile_picked_ema_none_e_kernel(tc, xT, mem, w1, old, new, offs, slot, out):
@@ -89,7 +90,7 @@ def tile_picked_ema_none_e_kernel(tc, xT, mem, w1, old, new, offs, slot, out):
         nc.vector.tensor_copy(picked[0][:, :, 1], planes[1][:].indirect(offs_first))
 
         rounded3 = keep.tile([P, T], BF16, name="rounded3")
-        for i, (c0, c1) in enumerate(CHUNKS):
+        for i, (c0, c1) in enumerate(ROUNDING):
             if i == 1:
                 nc.vector.tensor_copy(out=rounded3[:, c0:c1], in_=planes[3][:, c0:c1])
             else:

@@ -20,7 +20,7 @@ COPY = mybir.ActivationFunctionType.Copy
 
 HALF = S // 2
 GROUPS = S // P
-COPIED = 512
+COPIED = 704
 CHUNKS = ((0, 1536), (1536, 2048))
 ROUNDING = ((0, 512), (512, 1536), (1536, 2048))
 
@@ -52,6 +52,10 @@ def tile_picked_ema_none_e_kernel(tc, xT, mem, w1, old, new, offs, slot, out):
         nc.sync.dma_start(out=mem_sb[:, COPIED:], in_=mem[:, COPIED:])
         slot_sb = keep.tile([P, S // 16], U16, name="slot_sb")
         nc.sync.dma_start(slot_sb[:], slot)
+        new_first = keep.tile([P, P], F32, name="new_first")
+        nc.sync.dma_start(out=new_first[:], in_=new[:, 0:P])
+        old_last = keep.tile([P, P], F32, name="old_last")
+        nc.sync.dma_start(out=old_last[:], in_=old[:, S - P :])
         result = keep.tile([P, U], F32, name="result")
         nc.sync.dma_start(out=result[:, COPIED:], in_=mem[:, COPIED:])
 
@@ -71,8 +75,7 @@ def tile_picked_ema_none_e_kernel(tc, xT, mem, w1, old, new, offs, slot, out):
             nc.scalar.copy(out=full[:], in_=bank[:].rearrange("p c k -> p (c k)"))
             return full
 
-        old_all = spread(0, GROUPS, "old_all")
-        new_all = spread(GROUPS, 1, "new_all")
+        old_all = spread(0, GROUPS - 1, "old_all")
 
         picked = [keep.tile([P, HALF, PACK], BF16, name=f"picked{h}", align_bytes=64) for h in range(2)]
         offs_first = offs_sb[:, 0 : HALF // 16]
@@ -137,14 +140,13 @@ def tile_picked_ema_none_e_kernel(tc, xT, mem, w1, old, new, offs, slot, out):
 
         through_scalar([1], "rows_bank1", "turn_bank", "old_all_bank")
         quantise(1, "x_codes1", [slice(0, P), slice(P, HALF)])
-        kept_early = keep.tile([P, P], F32, name="kept_early")
-        nc.vector.tensor_tensor(kept_early[:], mem_sb[:].indirect(slots(early)), old_all[:, early], MULT)
+        kept = keep.tile([P, S], F32, name="kept")
+        nc.vector.tensor_tensor(kept[:, 0 : S - P], mem_sb[:].indirect(slots(slice(0, S - P))), old_all[:], MULT)
         added_early = keep.tile([P, P], F32, name="added_early")
-        nc.vector.tensor_tensor(added_early[:], y_bank[:], new_all[:], MULT)
+        nc.vector.tensor_tensor(added_early[:], y_bank[:], new_first[:], MULT)
         through_scalar([2], "rows_bank2", "rows_bank2", "back_bank2")
         through_scalar([3], "rows_bank3", "rows_bank3", "back_bank3")
-        kept_late = keep.tile([P, S - P], F32, name="kept_late", tag="plane3", align_bytes=64)
-        nc.vector.tensor_tensor(kept_late[:], mem_sb[:].indirect(slots(late)), old_all[:, late], MULT)
-        nc.vector.tensor_tensor(result[:].indirect(slots(early)), kept_early[:], added_early[:], ADD)
-        nc.vector.tensor_tensor(result[:].indirect(slots(late)), kept_late[:], added_late[:], ADD)
+        nc.vector.tensor_tensor(kept[:, S - P :], mem_sb[:].indirect(slots(slice(S - P, S))), old_last[:], MULT)
+        nc.vector.tensor_tensor(result[:].indirect(slots(early)), kept[:, early], added_early[:], ADD)
+        nc.vector.tensor_tensor(result[:].indirect(slots(late)), kept[:, late], added_late[:], ADD)
         nc.sync.dma_start(out=out, in_=result[:])

@@ -20,9 +20,10 @@ COPY = mybir.ActivationFunctionType.Copy
 
 HALF = S // 2
 GROUPS = S // P
+TURNED = GROUPS - 1
 COPIED = 704
 CHUNKS = ((0, 1536), (1536, 2048))
-ROUNDING = ((0, 512), (512, 1536), (1536, 2048))
+ROUNDING = ((0, 512), (512, 1536), (1536, 1664), (1664, 2048))
 
 
 def tile_picked_ema_none_e_kernel(tc, xT, mem, w1, old, new, offs, slot, out):
@@ -39,9 +40,9 @@ def tile_picked_ema_none_e_kernel(tc, xT, mem, w1, old, new, offs, slot, out):
         offs_sb = keep.tile([P, S // 16], U16, name="offs_sb")
         nc.sync.dma_start(out=planes[2][:], in_=x_rows[:, 2, :])
         nc.sync.dma_start(offs_sb[:], offs)
-        nc.sync.dma_start(out=flat[0:GROUPS, :], in_=old[0:1, :].rearrange("o (c p) -> (o c) p", p=P))
-        nc.sync.dma_start(out=flat[GROUPS : 2 * GROUPS, :], in_=new[0:1, :].rearrange("o (c p) -> (o c) p", p=P))
         nc.sync.dma_start(out=planes[0][:], in_=x_rows[:, 0, :])
+        nc.sync.dma_start(out=flat[0:TURNED, :], in_=old[0:1, 0 : S - P].rearrange("o (c p) -> (o c) p", p=P))
+        nc.sync.dma_start(out=flat[TURNED : 2 * TURNED, :], in_=new[0:1, P:].rearrange("o (c p) -> (o c) p", p=P))
         nc.sync.dma_start(out=planes[1][:], in_=x_rows[:, 1, :])
         for c0, c1 in CHUNKS:
             nc.sync.dma_start(out=planes[3][:, c0:c1], in_=x_rows[:, 3, c0:c1])
@@ -64,8 +65,8 @@ def tile_picked_ema_none_e_kernel(tc, xT, mem, w1, old, new, offs, slot, out):
 
         turn_bank = psum.tile([P, P], F32, name="turn_bank")
         nc.tensor.transpose(turn_bank[:], flat[:], ident[:])
-        by_row = keep.tile([P, 2 * GROUPS], F32, name="by_row")
-        nc.scalar.copy(out=by_row[:], in_=turn_bank[:, 0 : 2 * GROUPS])
+        by_row = keep.tile([P, 2 * TURNED], F32, name="by_row")
+        nc.scalar.copy(out=by_row[:], in_=turn_bank[:, 0 : 2 * TURNED])
 
         def spread(start, groups, name):
             bank = psum.tile([P, groups, P], F32, name=name + "_bank")
@@ -75,7 +76,7 @@ def tile_picked_ema_none_e_kernel(tc, xT, mem, w1, old, new, offs, slot, out):
             nc.scalar.copy(out=full[:], in_=bank[:].rearrange("p c k -> p (c k)"))
             return full
 
-        old_all = spread(0, GROUPS - 1, "old_all")
+        old_all = spread(0, TURNED, "old_all")
 
         picked = [keep.tile([P, HALF, PACK], BF16, name=f"picked{h}", align_bytes=64) for h in range(2)]
         offs_first = offs_sb[:, 0 : HALF // 16]
@@ -94,7 +95,7 @@ def tile_picked_ema_none_e_kernel(tc, xT, mem, w1, old, new, offs, slot, out):
 
         rounded3 = keep.tile([P, T], BF16, name="rounded3")
         for i, (c0, c1) in enumerate(ROUNDING):
-            if i == 1:
+            if i in (1, 2):
                 nc.vector.tensor_copy(out=rounded3[:, c0:c1], in_=planes[3][:, c0:c1])
             else:
                 nc.scalar.copy(out=rounded3[:, c0:c1], in_=planes[3][:, c0:c1])
@@ -132,14 +133,14 @@ def tile_picked_ema_none_e_kernel(tc, xT, mem, w1, old, new, offs, slot, out):
                 cols = slice(g % 2 * P, (g % 2 + 1) * P)
                 nc.tensor.matmul_mx(out=bank[:, i, :], lhsT=codes[g // 2][:, cols].bitcast(FP8X4), lhsT_scale=scales[g // 2][:, cols], rhs=w_codes[:].bitcast(FP8X4), rhs_scale=w_scales[:], start=True, stop=True)
             for i, g in enumerate(groups):
-                nc.scalar.activation(rows[:, g - 1, :], bank[:, i, :], COPY, scale=by_row[:, GROUPS + g : GROUPS + g + 1])
+                nc.scalar.activation(rows[:, g - 1, :], bank[:, i, :], COPY, scale=by_row[:, TURNED + g - 1 : TURNED + g])
             back = psum.tile([P, len(groups), P], F32, name=name + "_back", tag=back_tag)
             for i, g in enumerate(groups):
                 nc.tensor.transpose(back[:, i, :], rows[:, g - 1, :], ident[:])
             nc.scalar.copy(out=added_late[:, (groups[0] - 1) * P : groups[-1] * P], in_=back[:].rearrange("p c k -> p (c k)"))
 
         through_scalar([1], "rows_bank1", "turn_bank", "old_all_bank")
-        quantise(1, "x_codes1", [slice(0, P), slice(P, HALF)])
+        quantise(1, "picked0", [slice(0, P), slice(P, HALF)])
         kept = keep.tile([P, S], F32, name="kept")
         nc.vector.tensor_tensor(kept[:, 0 : S - P], mem_sb[:].indirect(slots(slice(0, S - P))), old_all[:], MULT)
         added_early = keep.tile([P, P], F32, name="added_early")

@@ -23,7 +23,7 @@ GROUPS = S // P
 TURNED = GROUPS - 1
 COPIED = 704
 CHUNKS = ((0, 1536), (1536, 2048))
-ROUNDING = ((0, 512), (512, 1536), (1536, 1664), (1664, 2048))
+ROUNDING = ((0, 512), (512, 1536), (1536, 1920), (1920, 2048))
 
 
 def tile_picked_ema_none_e_kernel(tc, xT, mem, w1, old, new, offs, slot, out):
@@ -95,8 +95,10 @@ def tile_picked_ema_none_e_kernel(tc, xT, mem, w1, old, new, offs, slot, out):
 
         rounded3 = keep.tile([P, T], BF16, name="rounded3")
         for i, (c0, c1) in enumerate(ROUNDING):
-            if i in (1, 2):
+            if i == 1:
                 nc.vector.tensor_copy(out=rounded3[:, c0:c1], in_=planes[3][:, c0:c1])
+            elif i == 3:
+                nc.gpsimd.tensor_scalar(rounded3[:, c0:c1], planes[3][:, c0:c1], 1.0, 0.0, MULT, ADD)
             else:
                 nc.scalar.copy(out=rounded3[:, c0:c1], in_=planes[3][:, c0:c1])
         nc.vector.tensor_copy(picked[0][:, :, 3], planes[3][:].indirect(offs_first))

@@ -22,6 +22,8 @@ HALF = S // 2
 GROUPS = S // P
 TURNED = GROUPS - 1
 COPIED = 704
+LAST_LOOKUP = 256
+OLD_TURNED = (S - LAST_LOOKUP) // P
 CHUNKS = ((0, 1536), (1536, 2048))
 ROUNDING = ((0, 512), (512, 1536), (1536, 1920), (1920, 2048))
 
@@ -41,8 +43,8 @@ def tile_picked_ema_none_e_kernel(tc, xT, mem, w1, old, new, offs, slot, out):
         nc.sync.dma_start(out=planes[2][:], in_=x_rows[:, 2, :])
         nc.sync.dma_start(offs_sb[:], offs)
         nc.sync.dma_start(out=planes[0][:], in_=x_rows[:, 0, :])
-        nc.sync.dma_start(out=flat[0:TURNED, :], in_=old[0:1, 0 : S - P].rearrange("o (c p) -> (o c) p", p=P))
-        nc.sync.dma_start(out=flat[TURNED : 2 * TURNED, :], in_=new[0:1, P:].rearrange("o (c p) -> (o c) p", p=P))
+        nc.sync.dma_start(out=flat[0:OLD_TURNED, :], in_=old[0:1, 0 : S - LAST_LOOKUP].rearrange("o (c p) -> (o c) p", p=P))
+        nc.sync.dma_start(out=flat[OLD_TURNED : OLD_TURNED + TURNED, :], in_=new[0:1, P:].rearrange("o (c p) -> (o c) p", p=P))
         nc.sync.dma_start(out=planes[1][:], in_=x_rows[:, 1, :])
         for c0, c1 in CHUNKS:
             nc.sync.dma_start(out=planes[3][:, c0:c1], in_=x_rows[:, 3, c0:c1])
@@ -55,8 +57,8 @@ def tile_picked_ema_none_e_kernel(tc, xT, mem, w1, old, new, offs, slot, out):
         nc.sync.dma_start(slot_sb[:], slot)
         new_first = keep.tile([P, P], F32, name="new_first")
         nc.sync.dma_start(out=new_first[:], in_=new[:, 0:P])
-        old_last = keep.tile([P, P], F32, name="old_last")
-        nc.sync.dma_start(out=old_last[:], in_=old[:, S - P :])
+        old_last = keep.tile([P, LAST_LOOKUP], F32, name="old_last")
+        nc.sync.dma_start(out=old_last[:], in_=old[:, S - LAST_LOOKUP :])
         result = keep.tile([P, U], F32, name="result")
         nc.sync.dma_start(out=result[:, COPIED:], in_=mem[:, COPIED:])
 
@@ -65,8 +67,8 @@ def tile_picked_ema_none_e_kernel(tc, xT, mem, w1, old, new, offs, slot, out):
 
         turn_bank = psum.tile([P, P], F32, name="turn_bank")
         nc.tensor.transpose(turn_bank[:], flat[:], ident[:])
-        by_row = keep.tile([P, 2 * TURNED], F32, name="by_row")
-        nc.scalar.copy(out=by_row[:], in_=turn_bank[:, 0 : 2 * TURNED])
+        by_row = keep.tile([P, OLD_TURNED + TURNED], F32, name="by_row")
+        nc.scalar.copy(out=by_row[:], in_=turn_bank[:, 0 : OLD_TURNED + TURNED])
 
         def spread(start, groups, name):
             bank = psum.tile([P, groups, P], F32, name=name + "_bank")
@@ -76,7 +78,7 @@ def tile_picked_ema_none_e_kernel(tc, xT, mem, w1, old, new, offs, slot, out):
             nc.scalar.copy(out=full[:], in_=bank[:].rearrange("p c k -> p (c k)"))
             return full
 
-        old_all = spread(0, TURNED, "old_all")
+        old_all = spread(0, OLD_TURNED, "old_all")
 
         picked = [keep.tile([P, HALF, PACK], BF16, name=f"picked{h}", align_bytes=64) for h in range(2)]
         offs_first = offs_sb[:, 0 : HALF // 16]
@@ -135,7 +137,7 @@ def tile_picked_ema_none_e_kernel(tc, xT, mem, w1, old, new, offs, slot, out):
                 cols = slice(g % 2 * P, (g % 2 + 1) * P)
                 nc.tensor.matmul_mx(out=bank[:, i, :], lhsT=codes[g // 2][:, cols].bitcast(FP8X4), lhsT_scale=scales[g // 2][:, cols], rhs=w_codes[:].bitcast(FP8X4), rhs_scale=w_scales[:], start=True, stop=True)
             for i, g in enumerate(groups):
-                nc.scalar.activation(rows[:, g - 1, :], bank[:, i, :], COPY, scale=by_row[:, TURNED + g - 1 : TURNED + g])
+                nc.scalar.activation(rows[:, g - 1, :], bank[:, i, :], COPY, scale=by_row[:, OLD_TURNED + g - 1 : OLD_TURNED + g])
             back = psum.tile([P, len(groups), P], F32, name=name + "_back", tag=back_tag)
             for i, g in enumerate(groups):
                 nc.tensor.transpose(back[:, i, :], rows[:, g - 1, :], ident[:])
@@ -144,12 +146,12 @@ def tile_picked_ema_none_e_kernel(tc, xT, mem, w1, old, new, offs, slot, out):
         through_scalar([1], "rows_bank1", "turn_bank", "old_all_bank")
         quantise(1, "picked0", [slice(0, P), slice(P, HALF)])
         kept = keep.tile([P, S], F32, name="kept")
-        nc.vector.tensor_tensor(kept[:, 0 : S - P], mem_sb[:].indirect(slots(slice(0, S - P))), old_all[:], MULT)
+        nc.vector.tensor_tensor(kept[:, 0 : S - LAST_LOOKUP], mem_sb[:].indirect(slots(slice(0, S - LAST_LOOKUP))), old_all[:, 0 : S - LAST_LOOKUP], MULT)
         added_early = keep.tile([P, P], F32, name="added_early")
         nc.vector.tensor_tensor(added_early[:], y_bank[:], new_first[:], MULT)
         through_scalar([2], "rows_bank2", "rows_bank2", "back_bank2")
         through_scalar([3], "rows_bank3", "rows_bank3", "back_bank3")
-        nc.vector.tensor_tensor(kept[:, S - P :], mem_sb[:].indirect(slots(slice(S - P, S))), old_last[:], MULT)
+        nc.vector.tensor_tensor(kept[:, S - LAST_LOOKUP :], mem_sb[:].indirect(slots(slice(S - LAST_LOOKUP, S))), old_last[:], MULT)
         nc.vector.tensor_tensor(result[:].indirect(slots(early)), kept[:, early], added_early[:], ADD)
         nc.vector.tensor_tensor(result[:].indirect(slots(late)), kept[:, late], added_late[:], ADD)
         nc.sync.dma_start(out=out, in_=result[:])

@@ -25,7 +25,7 @@ COPIED = 704
 LAST_LOOKUP = 256
 OLD_TURNED = (S - LAST_LOOKUP) // P
 CHUNKS = ((0, 1536), (1536, 2048))
-ROUNDING = ((0, 512), (512, 1536), (1536, 1920), (1920, 2048))
+ROUNDING = ((0, 512), (512, 1536), (1536, 1984), (1984, 2048))
 
 
 def tile_picked_ema_none_e_kernel(tc, xT, mem, w1, old, new, offs, slot, out):
@@ -97,10 +97,8 @@ def tile_picked_ema_none_e_kernel(tc, xT, mem, w1, old, new, offs, slot, out):
 
         rounded3 = keep.tile([P, T], BF16, name="rounded3")
         for i, (c0, c1) in enumerate(ROUNDING):
-            if i == 1:
+            if i % 2:
                 nc.vector.tensor_copy(out=rounded3[:, c0:c1], in_=planes[3][:, c0:c1])
-            elif i == 3:
-                nc.gpsimd.tensor_scalar(rounded3[:, c0:c1], planes[3][:, c0:c1], 1.0, 0.0, MULT, ADD)
             else:
                 nc.scalar.copy(out=rounded3[:, c0:c1], in_=planes[3][:, c0:c1])
         nc.vector.tensor_copy(picked[0][:, :, 3], planes[3][:].indirect(offs_first))

@@ -20,10 +20,6 @@ COPY = mybir.ActivationFunctionType.Copy
 
 HALF = S // 2
 GROUPS = S // P
-TURNED = GROUPS - 1
-COPIED = 704
-LAST_LOOKUP = 256
-OLD_TURNED = (S - LAST_LOOKUP) // P
 CHUNKS = ((0, 1536), (1536, 2048))
 ROUNDING = ((0, 512), (512, 1536), (1536, 1984), (1984, 2048))
 
@@ -43,51 +39,49 @@ def tile_picked_ema_none_e_kernel(tc, xT, mem, w1, old, new, offs, slot, out):
         nc.sync.dma_start(out=planes[2][:], in_=x_rows[:, 2, :])
         nc.sync.dma_start(offs_sb[:], offs)
         nc.sync.dma_start(out=planes[0][:], in_=x_rows[:, 0, :])
-        nc.sync.dma_start(out=flat[0:OLD_TURNED, :], in_=old[0:1, 0 : S - LAST_LOOKUP].rearrange("o (c p) -> (o c) p", p=P))
-        nc.sync.dma_start(out=flat[OLD_TURNED : OLD_TURNED + TURNED, :], in_=new[0:1, P:].rearrange("o (c p) -> (o c) p", p=P))
+        nc.sync.dma_start(out=flat[0:GROUPS, :], in_=old[0:1, :].rearrange("o (c p) -> (o c) p", p=P))
+        nc.sync.dma_start(out=flat[GROUPS : 2 * GROUPS, :], in_=new[0:1, :].rearrange("o (c p) -> (o c) p", p=P))
         nc.sync.dma_start(out=planes[1][:], in_=x_rows[:, 1, :])
         for c0, c1 in CHUNKS:
             nc.sync.dma_start(out=planes[3][:, c0:c1], in_=x_rows[:, 3, c0:c1])
         w_raw = keep.tile([P, PACK, N], F32, name="w_raw")
         nc.sync.dma_start(out=w_raw[:], in_=w1.rearrange("(p j) m -> p j m", j=PACK))
-        mem_sb = keep.tile([P, U], F32, name="mem_sb")
-        nc.sync.dma_start(out=mem_sb[:, 0:COPIED], in_=mem[:, 0:COPIED])
-        nc.sync.dma_start(out=mem_sb[:, COPIED:], in_=mem[:, COPIED:])
         slot_sb = keep.tile([P, S // 16], U16, name="slot_sb")
         nc.sync.dma_start(slot_sb[:], slot)
-        new_first = keep.tile([P, P], F32, name="new_first")
-        nc.sync.dma_start(out=new_first[:], in_=new[:, 0:P])
-        old_last = keep.tile([P, LAST_LOOKUP], F32, name="old_last")
-        nc.sync.dma_start(out=old_last[:], in_=old[:, S - LAST_LOOKUP :])
+        mem_sb = keep.tile([P, U], F32, name="mem_sb")
+        nc.sync.dma_start(out=mem_sb[:], in_=mem)
         result = keep.tile([P, U], F32, name="result")
-        nc.sync.dma_start(out=result[:, COPIED:], in_=mem[:, COPIED:])
+        nc.sync.dma_start(out=result[:], in_=mem)
 
         ident = keep.tile([P, P], F32, name="ident")
         make_identity(nc, ident[:])
 
         turn_bank = psum.tile([P, P], F32, name="turn_bank")
         nc.tensor.transpose(turn_bank[:], flat[:], ident[:])
-        by_row = keep.tile([P, OLD_TURNED + TURNED], F32, name="by_row")
-        nc.scalar.copy(out=by_row[:], in_=turn_bank[:, 0 : OLD_TURNED + TURNED])
+        by_row = keep.tile([P, 2 * GROUPS], F32, name="by_row")
+        nc.scalar.copy(out=by_row[:], in_=turn_bank[:, 0 : 2 * GROUPS])
 
-        def spread(start, groups, name):
-            bank = psum.tile([P, groups, P], F32, name=name + "_bank")
-            for c in range(groups):
-                nc.tensor.transpose(bank[:, c, :], by_row[:, start + c : start + c + 1].to_broadcast([P, P]), ident[:])
-            full = keep.tile([P, groups * P], F32, name=name)
-            nc.scalar.copy(out=full[:], in_=bank[:].rearrange("p c k -> p (c k)"))
-            return full
+        def spread(rows, name):
+            bank = psum.tile([P, len(rows) * P], F32, name=name)
+            for c, row in enumerate(rows):
+                nc.tensor.transpose(bank[:, c * P : (c + 1) * P], by_row[:, row : row + 1].to_broadcast([P, P]), ident[:])
+            return bank
 
-        old_all = spread(0, OLD_TURNED, "old_all")
+        early_bank = spread([0, 1, GROUPS, GROUPS + 1], "early_bank")
+        old_first = keep.tile([P, P], F32, name="old_first", align_bytes=64)
+        old_second = keep.tile([P, P], F32, name="old_second", align_bytes=64)
+        new_early = keep.tile([P, HALF], F32, name="new_early")
+        nc.scalar.copy(out=old_first[:], in_=early_bank[:, 0:P])
+        nc.scalar.copy(out=old_second[:], in_=early_bank[:, P:HALF])
+        nc.scalar.copy(out=new_early[:], in_=early_bank[:, HALF:])
+        old_last = spread([2, 3], "old_last")
 
         picked = [keep.tile([P, HALF, PACK], BF16, name=f"picked{h}", align_bytes=64) for h in range(2)]
         offs_first = offs_sb[:, 0 : HALF // 16]
         offs_second = offs_sb[:, HALF // 16 : S // 16]
 
         nc.vector.tensor_copy(picked[0][:, :, 2], planes[2][:].indirect(offs_first))
-        rounded2 = keep.tile([P, T], BF16, name="rounded2")
-        nc.scalar.copy(out=rounded2[:], in_=planes[2][:])
-        nc.scalar.activation(picked[1][:, :, 2], rounded2[:].indirect(offs_second), COPY)
+        nc.vector.tensor_copy(picked[1][:, :, 2], planes[2][:].indirect(offs_second))
 
         nc.vector.tensor_copy(picked[0][:, :, 0], planes[0][:].indirect(offs_first))
         nc.vector.tensor_copy(picked[1][:, :, 0], planes[0][:].indirect(offs_second))
@@ -106,7 +100,6 @@ def tile_picked_ema_none_e_kernel(tc, xT, mem, w1, old, new, offs, slot, out):
         nc.vector.tensor_copy(out=w_grouped[:].rearrange("p (c i) j -> p c j i", i=4), in_=w_raw[:].rearrange("p j (c i) -> p c j i", i=4))
         nc.scalar.activation(picked[1][:, :, 3], rounded3[:].indirect(offs_second), COPY)
 
-        nc.scalar.copy(out=result[:, 0:COPIED], in_=mem_sb[:, 0:COPIED])
         w_codes = keep.tile([P, N], U32, name="w_codes", align_bytes=64)
         w_scales = keep.tile([P, N], U8, name="w_scales", align_bytes=64)
         codes, scales = {}, {}
@@ -120,36 +113,33 @@ def tile_picked_ema_none_e_kernel(tc, xT, mem, w1, old, new, offs, slot, out):
         def slots(entries):
             return slot_sb[:, entries.start // 16 : entries.stop // 16]
 
-        early = slice(0, P)
-        late = slice(P, S)
-        quantise(0, "plane3", [slice(0, HALF)])
+        first, second = slice(0, P), slice(P, HALF)
+        early, late = slice(0, HALF), slice(HALF, S)
+        quantise(0, "plane3", [early])
         nc.vector.quantize_mx(out=w_codes[:].bitcast(FP8X4), scales=w_scales[:], in_=w_grouped[:].rearrange("p m j -> p (m j)"))
-        y_bank = psum.tile([P, P], F32, name="y_bank")
-        nc.tensor.matmul_mx(out=y_bank[:], lhsT=w_codes[:].bitcast(FP8X4), lhsT_scale=w_scales[:], rhs=codes[0][:, 0:P].bitcast(FP8X4), rhs_scale=scales[0][:, 0:P], start=True, stop=True)
-        rows = keep.tile([P, GROUPS - 1, N], F32, name="rows")
-        added_late = keep.tile([P, S - P], F32, name="added_late")
+        y_bank = psum.tile([P, HALF], F32, name="y_bank")
+        nc.tensor.matmul_mx(out=y_bank[:], lhsT=w_codes[:].bitcast(FP8X4), lhsT_scale=w_scales[:], rhs=codes[0][:].bitcast(FP8X4), rhs_scale=scales[0][:], start=True, stop=True)
 
-        def through_scalar(groups, name, tag, back_tag):
-            bank = psum.tile([P, len(groups), N], F32, name=name, tag=tag)
-            for i, g in enumerate(groups):
-                cols = slice(g % 2 * P, (g % 2 + 1) * P)
-                nc.tensor.matmul_mx(out=bank[:, i, :], lhsT=codes[g // 2][:, cols].bitcast(FP8X4), lhsT_scale=scales[g // 2][:, cols], rhs=w_codes[:].bitcast(FP8X4), rhs_scale=w_scales[:], start=True, stop=True)
-            for i, g in enumerate(groups):
-                nc.scalar.activation(rows[:, g - 1, :], bank[:, i, :], COPY, scale=by_row[:, OLD_TURNED + g - 1 : OLD_TURNED + g])
-            back = psum.tile([P, len(groups), P], F32, name=name + "_back", tag=back_tag)
-            for i, g in enumerate(groups):
-                nc.tensor.transpose(back[:, i, :], rows[:, g - 1, :], ident[:])
-            nc.scalar.copy(out=added_late[:, (groups[0] - 1) * P : groups[-1] * P], in_=back[:].rearrange("p c k -> p (c k)"))
-
-        through_scalar([1], "rows_bank1", "turn_bank", "old_all_bank")
-        quantise(1, "picked0", [slice(0, P), slice(P, HALF)])
-        kept = keep.tile([P, S], F32, name="kept")
-        nc.vector.tensor_tensor(kept[:, 0 : S - LAST_LOOKUP], mem_sb[:].indirect(slots(slice(0, S - LAST_LOOKUP))), old_all[:, 0 : S - LAST_LOOKUP], MULT)
-        added_early = keep.tile([P, P], F32, name="added_early")
-        nc.vector.tensor_tensor(added_early[:], y_bank[:], new_first[:], MULT)
-        through_scalar([2], "rows_bank2", "rows_bank2", "back_bank2")
-        through_scalar([3], "rows_bank3", "rows_bank3", "back_bank3")
-        nc.vector.tensor_tensor(kept[:, S - LAST_LOOKUP :], mem_sb[:].indirect(slots(slice(S - LAST_LOOKUP, S))), old_last[:], MULT)
-        nc.vector.tensor_tensor(result[:].indirect(slots(early)), kept[:, early], added_early[:], ADD)
-        nc.vector.tensor_tensor(result[:].indirect(slots(late)), kept[:, late], added_late[:], ADD)
+        kept_early = keep.tile([P, HALF], F32, name="kept_early")
+        nc.vector.tensor_tensor(kept_early[:, first], mem_sb[:].indirect(slots(first)), old_first[:], MULT)
+        nc.vector.tensor_tensor(kept_early[:, second], mem_sb[:].indirect(slots(second)), old_second[:], MULT)
+        found = keep.tile([P, HALF], F32, name="found")
+        nc.scalar.activation(found[:], mem_sb[:].indirect(slots(late)), COPY)
+        quantise(1, "old_first", [early])
+        weighed = keep.tile([P, S], F32, name="weighed", tag="old_second", align_bytes=64)
+        nc.vector.tensor_tensor(weighed[:, early], y_bank[:], new_early[:], MULT)
+        kept_late = keep.tile([P, HALF], F32, name="kept_late", tag="picked1", align_bytes=64)
+        nc.vector.tensor_tensor(kept_late[:], found[:], old_last[:], MULT)
+        added_late = keep.tile([P, HALF], F32, name="added_late")
+        for g in range(2, GROUPS):
+            cols = slice((g - 2) * P, (g - 1) * P)
+            rows = weighed[:, g * P : (g + 1) * P]
+            bank = psum.tile([P, N], F32, name=f"rows_bank{g}")
+            nc.tensor.matmul_mx(out=bank[:], lhsT=codes[1][:, cols].bitcast(FP8X4), lhsT_scale=scales[1][:, cols], rhs=w_codes[:].bitcast(FP8X4), rhs_scale=w_scales[:], start=True, stop=True)
+            nc.scalar.activation(rows, bank[:], COPY, scale=by_row[:, GROUPS + g : GROUPS + g + 1])
+            back = psum.tile([P, P], F32, name=f"back_bank{g}")
+            nc.tensor.transpose(back[:], rows, ident[:])
+            nc.scalar.copy(out=added_late[:, cols], in_=back[:])
+        nc.vector.tensor_tensor(result[:].indirect(slots(early)), kept_early[:], weighed[:, early], ADD)
+        nc.vector.tensor_tensor(result[:].indirect(slots(late)), kept_late[:], added_late[:], ADD)
         nc.sync.dma_start(out=out, in_=result[:])

@@ -50,8 +50,6 @@ def tile_picked_ema_none_e_kernel(tc, xT, mem, w1, old, new, offs, slot, out):
         nc.sync.dma_start(slot_sb[:], slot)
         mem_sb = keep.tile([P, U], F32, name="mem_sb")
         nc.sync.dma_start(out=mem_sb[:], in_=mem)
-        result = keep.tile([P, U], F32, name="result")
-        nc.sync.dma_start(out=result[:], in_=mem)
 
         ident = keep.tile([P, P], F32, name="ident")
         make_identity(nc, ident[:])
@@ -140,6 +138,6 @@ def tile_picked_ema_none_e_kernel(tc, xT, mem, w1, old, new, offs, slot, out):
             back = psum.tile([P, P], F32, name=f"back_bank{g}")
             nc.tensor.transpose(back[:], rows, ident[:])
             nc.scalar.copy(out=added_late[:, cols], in_=back[:])
-        nc.vector.tensor_tensor(result[:].indirect(slots(early)), kept_early[:], weighed[:, early], ADD)
-        nc.vector.tensor_tensor(result[:].indirect(slots(late)), kept_late[:], added_late[:], ADD)
-        nc.sync.dma_start(out=out, in_=result[:])
+        nc.vector.tensor_tensor(mem_sb[:].indirect(slots(early)), kept_early[:], weighed[:, early], ADD)
+        nc.vector.tensor_tensor(mem_sb[:].indirect(slots(late)), kept_late[:], added_late[:], ADD)
+        nc.sync.dma_start(out=out, in_=mem_sb[:])

@@ -21,7 +21,7 @@ COPY = mybir.ActivationFunctionType.Copy
 HALF = S // 2
 GROUPS = S // P
 CHUNKS = ((0, 1536), (1536, 2048))
-ROUNDING = ((0, 512), (512, 1536), (1536, 1984), (1984, 2048))
+ROUNDING = ((0, 512), (512, 1536), (1536, 2048))
 
 
 def tile_picked_ema_none_e_kernel(tc, xT, mem, w1, old, new, offs, slot, out):
@@ -39,8 +39,8 @@ def tile_picked_ema_none_e_kernel(tc, xT, mem, w1, old, new, offs, slot, out):
         nc.sync.dma_start(out=planes[2][:], in_=x_rows[:, 2, :])
         nc.sync.dma_start(offs_sb[:], offs)
         nc.sync.dma_start(out=planes[0][:], in_=x_rows[:, 0, :])
-        nc.sync.dma_start(out=flat[0:GROUPS, :], in_=old[0:1, :].rearrange("o (c p) -> (o c) p", p=P))
-        nc.sync.dma_start(out=flat[GROUPS : 2 * GROUPS, :], in_=new[0:1, :].rearrange("o (c p) -> (o c) p", p=P))
+        for i, values in enumerate((old[0:1, 0:HALF], new[0:1, 0:HALF], old[0:1, HALF:])):
+            nc.sync.dma_start(out=flat[2 * i : 2 * i + 2, :], in_=values.rearrange("o (c p) -> (o c) p", p=P))
         nc.sync.dma_start(out=planes[1][:], in_=x_rows[:, 1, :])
         for c0, c1 in CHUNKS:
             nc.sync.dma_start(out=planes[3][:, c0:c1], in_=x_rows[:, 3, c0:c1])
@@ -50,14 +50,19 @@ def tile_picked_ema_none_e_kernel(tc, xT, mem, w1, old, new, offs, slot, out):
         nc.sync.dma_start(slot_sb[:], slot)
         mem_sb = keep.tile([P, U], F32, name="mem_sb")
         nc.sync.dma_start(out=mem_sb[:], in_=mem)
+        new_columns = {}
+        for g in range(2, GROUPS):
+            new_columns[g] = keep.tile([P, 1], F32, name=f"new_column{g}")
+            with nc.allow_non_contiguous_dma(reason="one value a partition"):
+                nc.sync.dma_start(out=new_columns[g][:], in_=new[0:1, g * P : (g + 1) * P].rearrange("o p -> p o"))
 
         ident = keep.tile([P, P], F32, name="ident")
         make_identity(nc, ident[:])
 
         turn_bank = psum.tile([P, P], F32, name="turn_bank")
         nc.tensor.transpose(turn_bank[:], flat[:], ident[:])
-        by_row = keep.tile([P, 2 * GROUPS], F32, name="by_row")
-        nc.scalar.copy(out=by_row[:], in_=turn_bank[:, 0 : 2 * GROUPS])
+        by_row = keep.tile([P, 6], F32, name="by_row")
+        nc.scalar.copy(out=by_row[:], in_=turn_bank[:, 0 : 6])
 
         def spread(rows, name):
             bank = psum.tile([P, len(rows) * P], F32, name=name)
@@ -65,14 +70,14 @@ def tile_picked_ema_none_e_kernel(tc, xT, mem, w1, old, new, offs, slot, out):
                 nc.tensor.transpose(bank[:, c * P : (c + 1) * P], by_row[:, row : row + 1].to_broadcast([P, P]), ident[:])
             return bank
 
-        early_bank = spread([0, 1, GROUPS, GROUPS + 1], "early_bank")
+        early_bank = spread([0, 1, 2, 3], "early_bank")
         old_first = keep.tile([P, P], F32, name="old_first", align_bytes=64)
         old_second = keep.tile([P, P], F32, name="old_second", align_bytes=64)
         new_early = keep.tile([P, HALF], F32, name="new_early")
         nc.scalar.copy(out=old_first[:], in_=early_bank[:, 0:P])
         nc.scalar.copy(out=old_second[:], in_=early_bank[:, P:HALF])
         nc.scalar.copy(out=new_early[:], in_=early_bank[:, HALF:])
-        old_last = spread([2, 3], "old_last")
+        old_last = spread([4, 5], "old_last")
 
         picked = [keep.tile([P, HALF, PACK], BF16, name=f"picked{h}", align_bytes=64) for h in range(2)]
         offs_first = offs_sb[:, 0 : HALF // 16]
@@ -134,7 +139,7 @@ def tile_picked_ema_none_e_kernel(tc, xT, mem, w1, old, new, offs, slot, out):
             rows = weighed[:, g * P : (g + 1) * P]
             bank = psum.tile([P, N], F32, name=f"rows_bank{g}")
             nc.tensor.matmul_mx(out=bank[:], lhsT=codes[1][:, cols].bitcast(FP8X4), lhsT_scale=scales[1][:, cols], rhs=w_codes[:].bitcast(FP8X4), rhs_scale=w_scales[:], start=True, stop=True)
-            nc.scalar.activation(rows, bank[:], COPY, scale=by_row[:, GROUPS + g : GROUPS + g + 1])
+            nc.scalar.activation(rows, bank[:], COPY, scale=new_columns[g][:])
             back = psum.tile([P, P], F32, name=f"back_bank{g}")
             nc.tensor.transpose(back[:], rows, ident[:])
             nc.scalar.copy(out=added_late[:, cols], in_=back[:])

@@ -20,8 +20,6 @@ COPY = mybir.ActivationFunctionType.Copy
 
 HALF = S // 2
 GROUPS = S // P
-CHUNKS = ((0, 1536), (1536, 2048))
-ROUNDING = ((0, 512), (512, 1536), (1536, 2048))
 
 
 def tile_picked_ema_none_e_kernel(tc, xT, mem, w1, old, new, offs, slot, out):
@@ -36,14 +34,13 @@ def tile_picked_ema_none_e_kernel(tc, xT, mem, w1, old, new, offs, slot, out):
         flat = keep.tile([P, P], F32, name="flat")
         nc.gpsimd.memset(flat[:], 0.0)
         offs_sb = keep.tile([P, S // 16], U16, name="offs_sb")
-        nc.sync.dma_start(out=planes[2][:], in_=x_rows[:, 2, :])
-        nc.sync.dma_start(offs_sb[:], offs)
         nc.sync.dma_start(out=planes[0][:], in_=x_rows[:, 0, :])
-        for i, values in enumerate((old[0:1, 0:HALF], new[0:1, 0:HALF], old[0:1, HALF:])):
-            nc.sync.dma_start(out=flat[2 * i : 2 * i + 2, :], in_=values.rearrange("o (c p) -> (o c) p", p=P))
+        nc.sync.dma_start(offs_sb[:], offs)
         nc.sync.dma_start(out=planes[1][:], in_=x_rows[:, 1, :])
-        for c0, c1 in CHUNKS:
-            nc.sync.dma_start(out=planes[3][:, c0:c1], in_=x_rows[:, 3, c0:c1])
+        for first_row, values in ((0, old[0:1, 0:HALF]), (2, new[0:1, 0:HALF]), (4, old[0:1, HALF : HALF + P]), (5, old[0:1, HALF + P :])):
+            nc.sync.dma_start(out=flat[first_row : first_row + values.shape[1] // P, :], in_=values.rearrange("o (c p) -> (o c) p", p=P))
+        nc.sync.dma_start(out=planes[2][:], in_=x_rows[:, 2, :])
+        nc.sync.dma_start(out=planes[3][:], in_=x_rows[:, 3, :])
         w_raw = keep.tile([P, PACK, N], F32, name="w_raw")
         nc.sync.dma_start(out=w_raw[:], in_=w1.rearrange("(p j) m -> p j m", j=PACK))
         slot_sb = keep.tile([P, S // 16], U16, name="slot_sb")
@@ -62,7 +59,7 @@ def tile_picked_ema_none_e_kernel(tc, xT, mem, w1, old, new, offs, slot, out):
         turn_bank = psum.tile([P, P], F32, name="turn_bank")
         nc.tensor.transpose(turn_bank[:], flat[:], ident[:])
         by_row = keep.tile([P, 6], F32, name="by_row")
-        nc.scalar.copy(out=by_row[:], in_=turn_bank[:, 0 : 6])
+        nc.scalar.copy(out=by_row[:], in_=turn_bank[:, 0:6])
 
         def spread(rows, name):
             bank = psum.tile([P, len(rows) * P], F32, name=name)
@@ -74,52 +71,35 @@ def tile_picked_ema_none_e_kernel(tc, xT, mem, w1, old, new, offs, slot, out):
         old_first = keep.tile([P, P], F32, name="old_first", align_bytes=64)
         old_second = keep.tile([P, P], F32, name="old_second", align_bytes=64)
         new_early = keep.tile([P, HALF], F32, name="new_early")
-        nc.scalar.copy(out=old_first[:], in_=early_bank[:, 0:P])
-        nc.scalar.copy(out=old_second[:], in_=early_bank[:, P:HALF])
-        nc.scalar.copy(out=new_early[:], in_=early_bank[:, HALF:])
+        nc.vector.tensor_copy(out=old_first[:], in_=early_bank[:, 0:P])
+        nc.vector.tensor_copy(out=old_second[:], in_=early_bank[:, P:HALF])
+        nc.vector.tensor_copy(out=new_early[:], in_=early_bank[:, HALF:])
         old_last = spread([4, 5], "old_last")
 
         picked = [keep.tile([P, HALF, PACK], BF16, name=f"picked{h}", align_bytes=64) for h in range(2)]
-        offs_first = offs_sb[:, 0 : HALF // 16]
-        offs_second = offs_sb[:, HALF // 16 : S // 16]
+        offs_early = offs_sb[:, 0 : HALF // 16]
+        offs_late = offs_sb[:, HALF // 16 : S // 16]
+        for j in range(PACK):
+            nc.vector.tensor_copy(picked[0][:, :, j], planes[j][:].indirect(offs_early))
+            nc.scalar.activation(picked[1][:, :, j], planes[j][:].indirect(offs_late), COPY)
 
-        nc.vector.tensor_copy(picked[0][:, :, 2], planes[2][:].indirect(offs_first))
-        nc.vector.tensor_copy(picked[1][:, :, 2], planes[2][:].indirect(offs_second))
-
-        nc.vector.tensor_copy(picked[0][:, :, 0], planes[0][:].indirect(offs_first))
-        nc.vector.tensor_copy(picked[1][:, :, 0], planes[0][:].indirect(offs_second))
-
-        nc.vector.tensor_copy(picked[1][:, :, 1], planes[1][:].indirect(offs_second))
-        nc.vector.tensor_copy(picked[0][:, :, 1], planes[1][:].indirect(offs_first))
-
-        rounded3 = keep.tile([P, T], BF16, name="rounded3")
-        for i, (c0, c1) in enumerate(ROUNDING):
-            if i % 2:
-                nc.vector.tensor_copy(out=rounded3[:, c0:c1], in_=planes[3][:, c0:c1])
-            else:
-                nc.scalar.copy(out=rounded3[:, c0:c1], in_=planes[3][:, c0:c1])
-        nc.vector.tensor_copy(picked[0][:, :, 3], planes[3][:].indirect(offs_first))
         w_grouped = keep.tile([P, N, PACK], BF16, name="w_grouped", align_bytes=64)
-        nc.vector.tensor_copy(out=w_grouped[:].rearrange("p (c i) j -> p c j i", i=4), in_=w_raw[:].rearrange("p j (c i) -> p c j i", i=4))
-        nc.scalar.activation(picked[1][:, :, 3], rounded3[:].indirect(offs_second), COPY)
+        nc.scalar.copy(out=w_grouped[:].rearrange("p (c i) j -> p c j i", i=4), in_=w_raw[:].rearrange("p j (c i) -> p c j i", i=4))
 
+        codes, scales = {}, {}
+        for h in (1, 0):
+            codes[h] = keep.tile([P, HALF], U32, name=f"x_codes{h}", align_bytes=64)
+            scales[h] = keep.tile([P, HALF], U8, name=f"x_scales{h}", align_bytes=64)
+            nc.vector.quantize_mx(out=codes[h][:].bitcast(FP8X4), scales=scales[h][:], in_=picked[h][:].rearrange("p s j -> p (s j)"))
         w_codes = keep.tile([P, N], U32, name="w_codes", align_bytes=64)
         w_scales = keep.tile([P, N], U8, name="w_scales", align_bytes=64)
-        codes, scales = {}, {}
-
-        def quantise(h, tag, pieces):
-            codes[h] = keep.tile([P, HALF], U32, name=f"x_codes{h}", tag=tag, align_bytes=64)
-            scales[h] = keep.tile([P, HALF], U8, name=f"x_scales{h}", align_bytes=64)
-            for cols in pieces:
-                nc.vector.quantize_mx(out=codes[h][:, cols].bitcast(FP8X4), scales=scales[h][:, cols], in_=picked[h][:, cols, :].rearrange("p s j -> p (s j)"))
+        nc.vector.quantize_mx(out=w_codes[:].bitcast(FP8X4), scales=w_scales[:], in_=w_grouped[:].rearrange("p m j -> p (m j)"))
 
         def slots(entries):
             return slot_sb[:, entries.start // 16 : entries.stop // 16]
 
         first, second = slice(0, P), slice(P, HALF)
         early, late = slice(0, HALF), slice(HALF, S)
-        quantise(0, "plane3", [early])
-        nc.vector.quantize_mx(out=w_codes[:].bitcast(FP8X4), scales=w_scales[:], in_=w_grouped[:].rearrange("p m j -> p (m j)"))
         y_bank = psum.tile([P, HALF], F32, name="y_bank")
         nc.tensor.matmul_mx(out=y_bank[:], lhsT=w_codes[:].bitcast(FP8X4), lhsT_scale=w_scales[:], rhs=codes[0][:].bitcast(FP8X4), rhs_scale=scales[0][:], start=True, stop=True)
 
@@ -128,21 +108,20 @@ def tile_picked_ema_none_e_kernel(tc, xT, mem, w1, old, new, offs, slot, out):
         nc.vector.tensor_tensor(kept_early[:, second], mem_sb[:].indirect(slots(second)), old_second[:], MULT)
         found = keep.tile([P, HALF], F32, name="found")
         nc.scalar.activation(found[:], mem_sb[:].indirect(slots(late)), COPY)
-        quantise(1, "old_first", [early])
-        weighed = keep.tile([P, S], F32, name="weighed", tag="old_second", align_bytes=64)
-        nc.vector.tensor_tensor(weighed[:, early], y_bank[:], new_early[:], MULT)
-        kept_late = keep.tile([P, HALF], F32, name="kept_late", tag="picked1", align_bytes=64)
+        added_early = keep.tile([P, HALF], F32, name="added_early", tag="old_first", align_bytes=64)
+        nc.vector.tensor_tensor(added_early[:], y_bank[:], new_early[:], MULT)
+        kept_late = keep.tile([P, HALF], F32, name="kept_late", tag="old_second", align_bytes=64)
         nc.vector.tensor_tensor(kept_late[:], found[:], old_last[:], MULT)
         added_late = keep.tile([P, HALF], F32, name="added_late")
+        weighed = keep.tile([P, HALF], F32, name="weighed")
         for g in range(2, GROUPS):
             cols = slice((g - 2) * P, (g - 1) * P)
-            rows = weighed[:, g * P : (g + 1) * P]
             bank = psum.tile([P, N], F32, name=f"rows_bank{g}")
             nc.tensor.matmul_mx(out=bank[:], lhsT=codes[1][:, cols].bitcast(FP8X4), lhsT_scale=scales[1][:, cols], rhs=w_codes[:].bitcast(FP8X4), rhs_scale=w_scales[:], start=True, stop=True)
-            nc.scalar.activation(rows, bank[:], COPY, scale=new_columns[g][:])
+            nc.scalar.activation(weighed[:, cols], bank[:], COPY, scale=new_columns[g][:])
             back = psum.tile([P, P], F32, name=f"back_bank{g}")
-            nc.tensor.transpose(back[:], rows, ident[:])
+            nc.tensor.transpose(back[:], weighed[:, cols], ident[:])
             nc.scalar.copy(out=added_late[:, cols], in_=back[:])
-        nc.vector.tensor_tensor(mem_sb[:].indirect(slots(early)), kept_early[:], weighed[:, early], ADD)
+        nc.vector.tensor_tensor(mem_sb[:].indirect(slots(early)), kept_early[:], added_early[:], ADD)
         nc.vector.tensor_tensor(mem_sb[:].indirect(slots(late)), kept_late[:], added_late[:], ADD)
         nc.sync.dma_start(out=out, in_=mem_sb[:])

@@ -20,6 +20,7 @@ COPY = mybir.ActivationFunctionType.Copy
 
 HALF = S // 2
 GROUPS = S // P
+SPLIT = 320
 
 
 def tile_picked_ema_none_e_kernel(tc, xT, mem, w1, old, new, offs, slot, out):
@@ -37,7 +38,7 @@ def tile_picked_ema_none_e_kernel(tc, xT, mem, w1, old, new, offs, slot, out):
         nc.sync.dma_start(out=planes[0][:], in_=x_rows[:, 0, :])
         nc.sync.dma_start(offs_sb[:], offs)
         nc.sync.dma_start(out=planes[1][:], in_=x_rows[:, 1, :])
-        for first_row, values in ((0, old[0:1, 0:HALF]), (2, new[0:1, 0:HALF]), (4, old[0:1, HALF : HALF + P]), (5, old[0:1, HALF + P :])):
+        for first_row, values in ((0, old[0:1, 0:HALF]), (2, new[0:1, 0:P]), (3, new[0:1, P:HALF]), (4, old[0:1, HALF : HALF + P]), (5, old[0:1, HALF + P :])):
             nc.sync.dma_start(out=flat[first_row : first_row + values.shape[1] // P, :], in_=values.rearrange("o (c p) -> (o c) p", p=P))
         nc.sync.dma_start(out=planes[2][:], in_=x_rows[:, 2, :])
         nc.sync.dma_start(out=planes[3][:], in_=x_rows[:, 3, :])
@@ -76,21 +77,26 @@ def tile_picked_ema_none_e_kernel(tc, xT, mem, w1, old, new, offs, slot, out):
         nc.vector.tensor_copy(out=new_early[:], in_=early_bank[:, HALF:])
         old_last = spread([4, 5], "old_last")
 
-        picked = [keep.tile([P, HALF, PACK], BF16, name=f"picked{h}", align_bytes=64) for h in range(2)]
-        offs_early = offs_sb[:, 0 : HALF // 16]
-        offs_late = offs_sb[:, HALF // 16 : S // 16]
-        for j in range(PACK):
-            nc.vector.tensor_copy(picked[0][:, :, j], planes[j][:].indirect(offs_early))
-            nc.scalar.activation(picked[1][:, :, j], planes[j][:].indirect(offs_late), COPY)
+        picked = keep.tile([P, S, PACK], BF16, name="picked", align_bytes=64)
+
+        def messages(j, e0, e1):
+            return planes[j][:].indirect(offs_sb[:, e0 // 16 : e1 // 16])
+
+        for j in range(PACK - 1):
+            nc.vector.tensor_copy(picked[:, 0:SPLIT, j], messages(j, 0, SPLIT))
+            nc.scalar.activation(picked[:, SPLIT:, j], messages(j, SPLIT, S), COPY)
+        last = PACK - 1
+        nc.scalar.activation(picked[:, 3 * P :, last], messages(last, 3 * P, S), COPY)
+        nc.vector.tensor_copy(picked[:, 0:SPLIT, last], messages(last, 0, SPLIT))
+        nc.scalar.activation(picked[:, SPLIT : 3 * P, last], messages(last, SPLIT, 3 * P), COPY)
 
         w_grouped = keep.tile([P, N, PACK], BF16, name="w_grouped", align_bytes=64)
         nc.scalar.copy(out=w_grouped[:].rearrange("p (c i) j -> p c j i", i=4), in_=w_raw[:].rearrange("p j (c i) -> p c j i", i=4))
 
-        codes, scales = {}, {}
-        for h in (1, 0):
-            codes[h] = keep.tile([P, HALF], U32, name=f"x_codes{h}", align_bytes=64)
-            scales[h] = keep.tile([P, HALF], U8, name=f"x_scales{h}", align_bytes=64)
-            nc.vector.quantize_mx(out=codes[h][:].bitcast(FP8X4), scales=scales[h][:], in_=picked[h][:].rearrange("p s j -> p (s j)"))
+        codes = keep.tile([P, S], U32, name="x_codes", align_bytes=64)
+        scales = keep.tile([P, S], U8, name="x_scales", align_bytes=64)
+        for cols in (slice(3 * P, S), slice(0, HALF), slice(HALF, 3 * P)):
+            nc.vector.quantize_mx(out=codes[:, cols].bitcast(FP8X4), scales=scales[:, cols], in_=picked[:, cols, :].rearrange("p s j -> p (s j)"))
         w_codes = keep.tile([P, N], U32, name="w_codes", align_bytes=64)
         w_scales = keep.tile([P, N], U8, name="w_scales", align_bytes=64)
         nc.vector.quantize_mx(out=w_codes[:].bitcast(FP8X4), scales=w_scales[:], in_=w_grouped[:].rearrange("p m j -> p (m j)"))
@@ -101,7 +107,7 @@ def tile_picked_ema_none_e_kernel(tc, xT, mem, w1, old, new, offs, slot, out):
         first, second = slice(0, P), slice(P, HALF)
         early, late = slice(0, HALF), slice(HALF, S)
         y_bank = psum.tile([P, HALF], F32, name="y_bank")
-        nc.tensor.matmul_mx(out=y_bank[:], lhsT=w_codes[:].bitcast(FP8X4), lhsT_scale=w_scales[:], rhs=codes[0][:].bitcast(FP8X4), rhs_scale=scales[0][:], start=True, stop=True)
+        nc.tensor.matmul_mx(out=y_bank[:], lhsT=w_codes[:].bitcast(FP8X4), lhsT_scale=w_scales[:], rhs=codes[:, early].bitcast(FP8X4), rhs_scale=scales[:, early], start=True, stop=True)
 
         kept_early = keep.tile([P, HALF], F32, name="kept_early")
         nc.vector.tensor_tensor(kept_early[:, first], mem_sb[:].indirect(slots(first)), old_first[:], MULT)
@@ -117,7 +123,7 @@ def tile_picked_ema_none_e_kernel(tc, xT, mem, w1, old, new, offs, slot, out):
         for g in range(2, GROUPS):
             cols = slice((g - 2) * P, (g - 1) * P)
             bank = psum.tile([P, N], F32, name=f"rows_bank{g}")
-            nc.tensor.matmul_mx(out=bank[:], lhsT=codes[1][:, cols].bitcast(FP8X4), lhsT_scale=scales[1][:, cols], rhs=w_codes[:].bitcast(FP8X4), rhs_scale=w_scales[:], start=True, stop=True)
+            nc.tensor.matmul_mx(out=bank[:], lhsT=codes[:, g * P : (g + 1) * P].bitcast(FP8X4), lhsT_scale=scales[:, g * P : (g + 1) * P], rhs=w_codes[:].bitcast(FP8X4), rhs_scale=w_scales[:], start=True, stop=True)
             nc.scalar.activation(weighed[:, cols], bank[:], COPY, scale=new_columns[g][:])
             back = psum.tile([P, P], F32, name=f"back_bank{g}")
             nc.tensor.transpose(back[:], weighed[:, cols], ident[:])

@@ -72,9 +72,9 @@ def tile_picked_ema_none_e_kernel(tc, xT, mem, w1, old, new, offs, slot, out):
         old_first = keep.tile([P, P], F32, name="old_first", align_bytes=64)
         old_second = keep.tile([P, P], F32, name="old_second", align_bytes=64)
         new_early = keep.tile([P, HALF], F32, name="new_early")
-        nc.vector.tensor_copy(out=old_first[:], in_=early_bank[:, 0:P])
-        nc.vector.tensor_copy(out=old_second[:], in_=early_bank[:, P:HALF])
-        nc.vector.tensor_copy(out=new_early[:], in_=early_bank[:, HALF:])
+        nc.scalar.copy(out=old_first[:], in_=early_bank[:, 0:P])
+        nc.scalar.copy(out=old_second[:], in_=early_bank[:, P:HALF])
+        nc.scalar.copy(out=new_early[:], in_=early_bank[:, HALF:])
         old_last = spread([4, 5], "old_last")
 
         picked = keep.tile([P, S, PACK], BF16, name="picked", align_bytes=64)
@@ -82,9 +82,11 @@ def tile_picked_ema_none_e_kernel(tc, xT, mem, w1, old, new, offs, slot, out):
         def messages(j, e0, e1):
             return planes[j][:].indirect(offs_sb[:, e0 // 16 : e1 // 16])
 
-        for j in range(PACK - 1):
-            nc.vector.tensor_copy(picked[:, 0:SPLIT, j], messages(j, 0, SPLIT))
-            nc.scalar.activation(picked[:, SPLIT:, j], messages(j, SPLIT, S), COPY)
+        for j in range(2):
+            nc.vector.tensor_copy(picked[:, 0:HALF, j], messages(j, 0, HALF))
+            nc.vector.tensor_copy(picked[:, HALF:, j], messages(j, HALF, S))
+        nc.vector.tensor_copy(picked[:, 0:SPLIT, 2], messages(2, 0, SPLIT))
+        nc.scalar.activation(picked[:, SPLIT:, 2], messages(2, SPLIT, S), COPY)
         last = PACK - 1
         nc.scalar.activation(picked[:, 3 * P :, last], messages(last, 3 * P, S), COPY)
         nc.vector.tensor_copy(picked[:, 0:SPLIT, last], messages(last, 0, SPLIT))

@@ -38,11 +38,11 @@ def tile_picked_ema_none_e_kernel(tc, xT, mem, w1, old, new, offs, slot, out):
         nc.sync.dma_start(out=planes[0][:], in_=x_rows[:, 0, :])
         nc.sync.dma_start(offs_sb[:], offs)
         nc.sync.dma_start(out=planes[1][:], in_=x_rows[:, 1, :])
-        for first_row, values in ((0, old[0:1, 0:HALF]), (2, new[0:1, 0:P]), (3, new[0:1, P:HALF]), (4, old[0:1, HALF : HALF + P]), (5, old[0:1, HALF + P :])):
+        for first_row, values in ((0, old[0:1, 0:HALF]), (2, new[0:1, 0:HALF]), (4, old[0:1, HALF : HALF + P]), (5, old[0:1, HALF + P :])):
             nc.sync.dma_start(out=flat[first_row : first_row + values.shape[1] // P, :], in_=values.rearrange("o (c p) -> (o c) p", p=P))
         nc.sync.dma_start(out=planes[2][:], in_=x_rows[:, 2, :])
         nc.sync.dma_start(out=planes[3][:], in_=x_rows[:, 3, :])
-        w_raw = keep.tile([P, PACK, N], F32, name="w_raw")
+        w_raw = keep.tile([P, PACK, N], F32, name="w_raw", align_bytes=64)
         nc.sync.dma_start(out=w_raw[:], in_=w1.rearrange("(p j) m -> p j m", j=PACK))
         slot_sb = keep.tile([P, S // 16], U16, name="slot_sb")
         nc.sync.dma_start(slot_sb[:], slot)
@@ -95,21 +95,29 @@ def tile_picked_ema_none_e_kernel(tc, xT, mem, w1, old, new, offs, slot, out):
         w_grouped = keep.tile([P, N, PACK], BF16, name="w_grouped", align_bytes=64)
         nc.scalar.copy(out=w_grouped[:].rearrange("p (c i) j -> p c j i", i=4), in_=w_raw[:].rearrange("p j (c i) -> p c j i", i=4))
 
-        codes = keep.tile([P, S], U32, name="x_codes", align_bytes=64)
-        scales = keep.tile([P, S], U8, name="x_scales", align_bytes=64)
-        for cols in (slice(3 * P, S), slice(0, HALF), slice(HALF, 3 * P)):
-            nc.vector.quantize_mx(out=codes[:, cols].bitcast(FP8X4), scales=scales[:, cols], in_=picked[:, cols, :].rearrange("p s j -> p (s j)"))
+        def quantise(entries, tag):
+            width = entries.stop - entries.start
+            codes = keep.tile([P, width], U32, name=f"x_codes{entries.start}", align_bytes=64)
+            scales = keep.tile([P, width], U8, name=f"x_scales{entries.start}", tag=tag, align_bytes=64)
+            nc.vector.quantize_mx(out=codes[:].bitcast(FP8X4), scales=scales[:], in_=picked[:, entries, :].rearrange("p s j -> p (s j)"))
+            return codes, scales
+
+        late_groups = {3: quantise(slice(3 * P, S), "scales_last")}
+        early_codes, early_scales = quantise(slice(0, HALF), "scales_early")
         w_codes = keep.tile([P, N], U32, name="w_codes", align_bytes=64)
         w_scales = keep.tile([P, N], U8, name="w_scales", align_bytes=64)
         nc.vector.quantize_mx(out=w_codes[:].bitcast(FP8X4), scales=w_scales[:], in_=w_grouped[:].rearrange("p m j -> p (m j)"))
+        late_groups[2] = quantise(slice(HALF, 3 * P), "w_raw")
 
         def slots(entries):
             return slot_sb[:, entries.start // 16 : entries.stop // 16]
 
         first, second = slice(0, P), slice(P, HALF)
         early, late = slice(0, HALF), slice(HALF, S)
-        y_bank = psum.tile([P, HALF], F32, name="y_bank")
-        nc.tensor.matmul_mx(out=y_bank[:], lhsT=w_codes[:].bitcast(FP8X4), lhsT_scale=w_scales[:], rhs=codes[:, early].bitcast(FP8X4), rhs_scale=scales[:, early], start=True, stop=True)
+        y_banks = []
+        for cols, tag in ((first, "turn_bank"), (second, "y_second")):
+            y_banks.append(psum.tile([P, P], F32, name=f"y_bank{cols.start}", tag=tag))
+            nc.tensor.matmul_mx(out=y_banks[-1][:], lhsT=w_codes[:].bitcast(FP8X4), lhsT_scale=w_scales[:], rhs=early_codes[:, cols].bitcast(FP8X4), rhs_scale=early_scales[:, cols], start=True, stop=True)
 
         kept_early = keep.tile([P, HALF], F32, name="kept_early")
         nc.vector.tensor_tensor(kept_early[:, first], mem_sb[:].indirect(slots(first)), old_first[:], MULT)
@@ -117,15 +125,16 @@ def tile_picked_ema_none_e_kernel(tc, xT, mem, w1, old, new, offs, slot, out):
         found = keep.tile([P, HALF], F32, name="found")
         nc.scalar.activation(found[:], mem_sb[:].indirect(slots(late)), COPY)
         added_early = keep.tile([P, HALF], F32, name="added_early", tag="old_first", align_bytes=64)
-        nc.vector.tensor_tensor(added_early[:], y_bank[:], new_early[:], MULT)
+        for cols, y_bank in zip((first, second), y_banks):
+            nc.vector.tensor_tensor(added_early[:, cols], y_bank[:], new_early[:, cols], MULT)
         kept_late = keep.tile([P, HALF], F32, name="kept_late", tag="old_second", align_bytes=64)
         nc.vector.tensor_tensor(kept_late[:], found[:], old_last[:], MULT)
         added_late = keep.tile([P, HALF], F32, name="added_late")
         weighed = keep.tile([P, HALF], F32, name="weighed")
-        for g in range(2, GROUPS):
+        for g in (3, 2):
             cols = slice((g - 2) * P, (g - 1) * P)
             bank = psum.tile([P, N], F32, name=f"rows_bank{g}")
-            nc.tensor.matmul_mx(out=bank[:], lhsT=codes[:, g * P : (g + 1) * P].bitcast(FP8X4), lhsT_scale=scales[:, g * P : (g + 1) * P], rhs=w_codes[:].bitcast(FP8X4), rhs_scale=w_scales[:], start=True, stop=True)
+            nc.tensor.matmul_mx(out=bank[:], lhsT=late_groups[g][0][:].bitcast(FP8X4), lhsT_scale=late_groups[g][1][:], rhs=w_codes[:].bitcast(FP8X4), rhs_scale=w_scales[:], start=True, stop=True)
             nc.scalar.activation(weighed[:, cols], bank[:], COPY, scale=new_columns[g][:])
             back = psum.tile([P, P], F32, name=f"back_bank{g}")
             nc.tensor.transpose(back[:], weighed[:, cols], ident[:])

@@ -20,7 +20,7 @@ COPY = mybir.ActivationFunctionType.Copy
 
 HALF = S // 2
 GROUPS = S // P
-SPLIT = 320
+SPLIT = 288
 
 
 def tile_picked_ema_none_e_kernel(tc, xT, mem, w1, old, new, offs, slot, out):

@@ -20,7 +20,8 @@ COPY = mybir.ActivationFunctionType.Copy
 
 HALF = S // 2
 GROUPS = S // P
-SPLIT = 288
+SPLIT = 256
+FUSED = 320
 
 
 def tile_picked_ema_none_e_kernel(tc, xT, mem, w1, old, new, offs, slot, out):
@@ -70,12 +71,13 @@ def tile_picked_ema_none_e_kernel(tc, xT, mem, w1, old, new, offs, slot, out):
 
         early_bank = spread([0, 1, 2, 3], "early_bank")
         old_first = keep.tile([P, P], F32, name="old_first", align_bytes=64)
-        old_second = keep.tile([P, P], F32, name="old_second", align_bytes=64)
+        old_second = keep.tile([P, FUSED - P], F32, name="old_second", align_bytes=64)
         new_early = keep.tile([P, HALF], F32, name="new_early")
         nc.scalar.copy(out=old_first[:], in_=early_bank[:, 0:P])
-        nc.scalar.copy(out=old_second[:], in_=early_bank[:, P:HALF])
+        nc.scalar.copy(out=old_second[:, 0:P], in_=early_bank[:, P:HALF])
         nc.scalar.copy(out=new_early[:], in_=early_bank[:, HALF:])
         old_last = spread([4, 5], "old_last")
+        nc.scalar.copy(out=old_second[:, P:], in_=old_last[:, 0 : FUSED - HALF])
 
         picked = keep.tile([P, S, PACK], BF16, name="picked", align_bytes=64)
 
@@ -104,10 +106,10 @@ def tile_picked_ema_none_e_kernel(tc, xT, mem, w1, old, new, offs, slot, out):
 
         late_groups = {3: quantise(slice(3 * P, S), "scales_last")}
         early_codes, early_scales = quantise(slice(0, HALF), "scales_early")
+        late_groups[2] = quantise(slice(HALF, 3 * P), "scales_third")
         w_codes = keep.tile([P, N], U32, name="w_codes", align_bytes=64)
         w_scales = keep.tile([P, N], U8, name="w_scales", align_bytes=64)
         nc.vector.quantize_mx(out=w_codes[:].bitcast(FP8X4), scales=w_scales[:], in_=w_grouped[:].rearrange("p m j -> p (m j)"))
-        late_groups[2] = quantise(slice(HALF, 3 * P), "w_raw")
 
         def slots(entries):
             return slot_sb[:, entries.start // 16 : entries.stop // 16]
@@ -119,16 +121,15 @@ def tile_picked_ema_none_e_kernel(tc, xT, mem, w1, old, new, offs, slot, out):
             y_banks.append(psum.tile([P, P], F32, name=f"y_bank{cols.start}", tag=tag))
             nc.tensor.matmul_mx(out=y_banks[-1][:], lhsT=w_codes[:].bitcast(FP8X4), lhsT_scale=w_scales[:], rhs=early_codes[:, cols].bitcast(FP8X4), rhs_scale=early_scales[:, cols], start=True, stop=True)
 
-        kept_early = keep.tile([P, HALF], F32, name="kept_early")
-        nc.vector.tensor_tensor(kept_early[:, first], mem_sb[:].indirect(slots(first)), old_first[:], MULT)
-        nc.vector.tensor_tensor(kept_early[:, second], mem_sb[:].indirect(slots(second)), old_second[:], MULT)
-        found = keep.tile([P, HALF], F32, name="found")
-        nc.scalar.activation(found[:], mem_sb[:].indirect(slots(late)), COPY)
+        kept = keep.tile([P, S], F32, name="kept")
+        nc.vector.tensor_tensor(kept[:, first], mem_sb[:].indirect(slots(first)), old_first[:], MULT)
+        nc.vector.tensor_tensor(kept[:, P:FUSED], mem_sb[:].indirect(slots(slice(P, FUSED))), old_second[:], MULT)
+        found = keep.tile([P, S - FUSED], F32, name="found")
+        nc.scalar.activation(found[:], mem_sb[:].indirect(slots(slice(FUSED, S))), COPY)
         added_early = keep.tile([P, HALF], F32, name="added_early", tag="old_first", align_bytes=64)
         for cols, y_bank in zip((first, second), y_banks):
             nc.vector.tensor_tensor(added_early[:, cols], y_bank[:], new_early[:, cols], MULT)
-        kept_late = keep.tile([P, HALF], F32, name="kept_late", tag="old_second", align_bytes=64)
-        nc.vector.tensor_tensor(kept_late[:], found[:], old_last[:], MULT)
+        nc.vector.tensor_tensor(kept[:, FUSED:], found[:], old_last[:, FUSED - HALF :], MULT)
         added_late = keep.tile([P, HALF], F32, name="added_late")
         weighed = keep.tile([P, HALF], F32, name="weighed")
         for g in (3, 2):
@@ -139,6 +140,6 @@ def tile_picked_ema_none_e_kernel(tc, xT, mem, w1, old, new, offs, slot, out):
             back = psum.tile([P, P], F32, name=f"back_bank{g}")
             nc.tensor.transpose(back[:], weighed[:, cols], ident[:])
             nc.scalar.copy(out=added_late[:, cols], in_=back[:])
-        nc.vector.tensor_tensor(mem_sb[:].indirect(slots(early)), kept_early[:], added_early[:], ADD)
-        nc.vector.tensor_tensor(mem_sb[:].indirect(slots(late)), kept_late[:], added_late[:], ADD)
+        nc.vector.tensor_tensor(mem_sb[:].indirect(slots(early)), kept[:, early], added_early[:], ADD)
+        nc.vector.tensor_tensor(mem_sb[:].indirect(slots(late)), kept[:, late], added_late[:], ADD)
         nc.sync.dma_start(out=out, in_=mem_sb[:])

from contextlib import ExitStack

import concourse.mybir as mybir
from concourse.masks import make_identity

K, T, S, N, U = 512, 2048, 512, 128, 1024
P = 128
PACK = 4
FLOPS = 2 * K * N * S

F32 = mybir.dt.float32
BF16 = mybir.dt.bfloat16
U32 = mybir.dt.uint32
U16 = mybir.dt.uint16
U8 = mybir.dt.uint8
FP8X4 = mybir.dt.float8_e4m3fn_x4
MULT = mybir.AluOpType.mult
ADD = mybir.AluOpType.add
COPY = mybir.ActivationFunctionType.Copy

HALF = S // 2
GROUPS = S // P
SPLIT = 256
FUSED = 320


def tile_picked_ema_none_e_kernel(tc, xT, mem, w1, old, new, offs, slot, out):
    nc = tc.nc
    with ExitStack() as ctx:
        keep = ctx.enter_context(tc.tile_pool(name="keep", bufs=1))
        psum = ctx.enter_context(tc.psum_pool(name="psum", bufs=1))

        x_rows = xT.rearrange("(p j) t -> p j t", j=PACK)
        planes = [keep.tile([P, T], F32, name=f"plane{j}", align_bytes=64) for j in range(PACK)]

        flat = keep.tile([P, P], F32, name="flat")
        nc.gpsimd.memset(flat[:], 0.0)
        offs_sb = keep.tile([P, S // 16], U16, name="offs_sb")
        nc.sync.dma_start(out=planes[0][:], in_=x_rows[:, 0, :])
        nc.sync.dma_start(offs_sb[:], offs)
        nc.sync.dma_start(out=planes[1][:], in_=x_rows[:, 1, :])
        for first_row, values in ((0, old[0:1, 0:HALF]), (2, new[0:1, 0:HALF]), (4, old[0:1, HALF : HALF + P]), (5, old[0:1, HALF + P :])):
            nc.sync.dma_start(out=flat[first_row : first_row + values.shape[1] // P, :], in_=values.rearrange("o (c p) -> (o c) p", p=P))
        nc.sync.dma_start(out=planes[2][:], in_=x_rows[:, 2, :])
        nc.sync.dma_start(out=planes[3][:], in_=x_rows[:, 3, :])
        w_raw = keep.tile([P, PACK, N], F32, name="w_raw", align_bytes=64)
        nc.sync.dma_start(out=w_raw[:], in_=w1.rearrange("(p j) m -> p j m", j=PACK))
        slot_sb = keep.tile([P, S // 16], U16, name="slot_sb")
        nc.sync.dma_start(slot_sb[:], slot)
        mem_sb = keep.tile([P, U], F32, name="mem_sb")
        nc.sync.dma_start(out=mem_sb[:], in_=mem)
        new_columns = {}
        for g in range(2, GROUPS):
            new_columns[g] = keep.tile([P, 1], F32, name=f"new_column{g}")
            with nc.allow_non_contiguous_dma(reason="one value a partition"):
                nc.sync.dma_start(out=new_columns[g][:], in_=new[0:1, g * P : (g + 1) * P].rearrange("o p -> p o"))

        ident = keep.tile([P, P], F32, name="ident")
        make_identity(nc, ident[:])

        turn_bank = psum.tile([P, P], F32, name="turn_bank")
        nc.tensor.transpose(turn_bank[:], flat[:], ident[:])
        by_row = keep.tile([P, 6], F32, name="by_row")
        nc.scalar.copy(out=by_row[:], in_=turn_bank[:, 0:6])

        def spread(rows, name):
            bank = psum.tile([P, len(rows) * P], F32, name=name)
            for c, row in enumerate(rows):
                nc.tensor.transpose(bank[:, c * P : (c + 1) * P], by_row[:, row : row + 1].to_broadcast([P, P]), ident[:])
            return bank

        early_bank = spread([0, 1, 2, 3], "early_bank")
        old_first = keep.tile([P, P], F32, name="old_first", align_bytes=64)
        old_second = keep.tile([P, FUSED - P], F32, name="old_second", align_bytes=64)
        new_early = keep.tile([P, HALF], F32, name="new_early")
        nc.scalar.copy(out=old_first[:], in_=early_bank[:, 0:P])
        nc.scalar.copy(out=old_second[:, 0:P], in_=early_bank[:, P:HALF])
        nc.scalar.copy(out=new_early[:], in_=early_bank[:, HALF:])
        old_last = spread([4, 5], "old_last")
        nc.scalar.copy(out=old_second[:, P:], in_=old_last[:, 0 : FUSED - HALF])

        picked = keep.tile([P, S, PACK], BF16, name="picked", align_bytes=64)

        def messages(j, e0, e1):
            return planes[j][:].indirect(offs_sb[:, e0 // 16 : e1 // 16])

        for j in range(2):
            nc.vector.tensor_copy(picked[:, 0:HALF, j], messages(j, 0, HALF))
            nc.vector.tensor_copy(picked[:, HALF:, j], messages(j, HALF, S))
        nc.vector.tensor_copy(picked[:, 0:SPLIT, 2], messages(2, 0, SPLIT))
        nc.scalar.activation(picked[:, SPLIT:, 2], messages(2, SPLIT, S), COPY)
        last = PACK - 1
        nc.scalar.activation(picked[:, 3 * P :, last], messages(last, 3 * P, S), COPY)
        nc.vector.tensor_copy(picked[:, 0:SPLIT, last], messages(last, 0, SPLIT))
        nc.scalar.activation(picked[:, SPLIT : 3 * P, last], messages(last, SPLIT, 3 * P), COPY)

        w_grouped = keep.tile([P, N, PACK], BF16, name="w_grouped", align_bytes=64)
        nc.scalar.copy(out=w_grouped[:].rearrange("p (c i) j -> p c j i", i=4), in_=w_raw[:].rearrange("p j (c i) -> p c j i", i=4))

        def quantise(entries, tag):
            width = entries.stop - entries.start
            codes = keep.tile([P, width], U32, name=f"x_codes{entries.start}", align_bytes=64)
            scales = keep.tile([P, width], U8, name=f"x_scales{entries.start}", tag=tag, align_bytes=64)
            nc.vector.quantize_mx(out=codes[:].bitcast(FP8X4), scales=scales[:], in_=picked[:, entries, :].rearrange("p s j -> p (s j)"))
            return codes, scales

        late_groups = {3: quantise(slice(3 * P, S), "scales_last")}
        early_codes, early_scales = quantise(slice(0, HALF), "scales_early")
        late_groups[2] = quantise(slice(HALF, 3 * P), "scales_third")
        w_codes = keep.tile([P, N], U32, name="w_codes", align_bytes=64)
        w_scales = keep.tile([P, N], U8, name="w_scales", align_bytes=64)
        nc.vector.quantize_mx(out=w_codes[:].bitcast(FP8X4), scales=w_scales[:], in_=w_grouped[:].rearrange("p m j -> p (m j)"))

        def slots(entries):
            return slot_sb[:, entries.start // 16 : entries.stop // 16]

        first, second = slice(0, P), slice(P, HALF)
        early, late = slice(0, HALF), slice(HALF, S)
        y_banks = []
        for cols, tag in ((first, "turn_bank"), (second, "y_second")):
            y_banks.append(psum.tile([P, P], F32, name=f"y_bank{cols.start}", tag=tag))
            nc.tensor.matmul_mx(out=y_banks[-1][:], lhsT=w_codes[:].bitcast(FP8X4), lhsT_scale=w_scales[:], rhs=early_codes[:, cols].bitcast(FP8X4), rhs_scale=early_scales[:, cols], start=True, stop=True)

        kept = keep.tile([P, S], F32, name="kept")
        nc.vector.tensor_tensor(kept[:, first], mem_sb[:].indirect(slots(first)), old_first[:], MULT)
        nc.vector.tensor_tensor(kept[:, P:FUSED], mem_sb[:].indirect(slots(slice(P, FUSED))), old_second[:], MULT)
        found = keep.tile([P, S - FUSED], F32, name="found")
        nc.scalar.activation(found[:], mem_sb[:].indirect(slots(slice(FUSED, S))), COPY)
        added_early = keep.tile([P, HALF], F32, name="added_early", tag="old_first", align_bytes=64)
        for cols, y_bank in zip((first, second), y_banks):
            nc.vector.tensor_tensor(added_early[:, cols], y_bank[:], new_early[:, cols], MULT)
        nc.vector.tensor_tensor(kept[:, FUSED:], found[:], old_last[:, FUSED - HALF :], MULT)
        added_late = keep.tile([P, HALF], F32, name="added_late")
        weighed = keep.tile([P, HALF], F32, name="weighed")
        for g in (3, 2):
            cols = slice((g - 2) * P, (g - 1) * P)
            bank = psum.tile([P, N], F32, name=f"rows_bank{g}")
            nc.tensor.matmul_mx(out=bank[:], lhsT=late_groups[g][0][:].bitcast(FP8X4), lhsT_scale=late_groups[g][1][:], rhs=w_codes[:].bitcast(FP8X4), rhs_scale=w_scales[:], start=True, stop=True)
            nc.scalar.activation(weighed[:, cols], bank[:], COPY, scale=new_columns[g][:])
            back = psum.tile([P, P], F32, name=f"back_bank{g}")
            nc.tensor.transpose(back[:], weighed[:, cols], ident[:])
            nc.scalar.copy(out=added_late[:, cols], in_=back[:])
        nc.vector.tensor_tensor(mem_sb[:].indirect(slots(early)), kept[:, early], added_early[:], ADD)
        nc.vector.tensor_tensor(mem_sb[:].indirect(slots(late)), kept[:, late], added_late[:], ADD)
        nc.sync.dma_start(out=out, in_=mem_sb[:])
